import numpy as np, ml_dtypes
CORES = [10,34,74,98]
N = 4
BF = ml_dtypes.bfloat16
def gentries(a):
    return np.ascontiguousarray(a.reshape(8, 16, -1).transpose(0, 2, 1)).reshape(8, -1)
def gtable(e):
    e = np.asarray(e); return np.ascontiguousarray(e.reshape(8, -1, 16).transpose(0, 2, 1)).reshape(128, -1).astype(np.int32)
W, V, KC, R = 4096, 2048, 64, 3
LO, HI = 40, 250
def peps(rng):
    p = rng.integers(LO, HI + 1, (N, 8, V, 16)); i = np.arange(16); s = rng.integers(0, 15, (N, 8, V // 2, 1))
    p[:, :, 1::2] = np.take_along_axis(p[:, :, 0::2], np.where(i == s, s + 1, np.where(i == s + 1, s, i)), axis=-1); return p
def wants(rng):
    w = rng.integers(0, V, (N, 8, N, KC)); w[..., 1::2] = np.where(rng.random((N, 8, N, KC // 2)) < 0.25, w[..., 0::2] ^ 1, w[..., 1::2])
    w[..., KC - 1] = w[..., 2]; return w
def own(rng):
    e = np.argsort(rng.random((N, 8, V // 2)), axis=-1)[:, :, :N * KC // 2]; x = rng.integers(0, 2, e.shape)
    return np.stack([2 * e + x, 2 * e + 1 - x], axis=-1).reshape(N, 8, N, KC).transpose(2, 1, 0, 3).copy()
def bins(p, w):
    m = p[np.arange(N)[None, None, :, None], np.arange(8)[None, :, None, None], w].reshape(N, 8, N * KC, 16)
    b = np.add.accumulate(m, axis=-1); return b, b[..., -1:] + 64 - b
def noise(rng):
    return rng.integers(1, 4, (N, 8, 16, W)) * (rng.random((N, 8, 16, W)) < 0.3)
def some(rng):
    return np.argsort(rng.random((N, 8, N * KC)), axis=-1)[..., :R + 1]
def shine(rng, s, b, y, n, a, z):
    for r in range(N):
        for g in range(8):
            for t in n[r, g]:
                s[r, g][:, b[r, g, t]] = rng.integers(a, z + 1, (16, 16)); s[r, g][:, y[r, g, t]] = rng.integers(a, z + 1, (16, 16))
def pack(s, p, w):
    return {"spec": s.reshape(N, 128, W).astype(np.float32).astype(BF), "pep": p.transpose(0, 1, 3, 2).reshape(N, 128, V).astype(np.float32).astype(BF),
            "want": np.stack([gtable(w[r].reshape(8, N * KC)) for r in range(N)])}
def setup_inputs(rng):
    p, w, s, n = peps(rng), wants(rng), noise(rng), some(rng); b, y = bins(p, w)
    n[:, ::2, 0] = KC * rng.integers(0, N, (N, 4)) + 2; shine(rng, s, b, y, n, 4, 15)
    return pack(s, p, w)
def setup_inputs_kin(rng):
    p, w, s = peps(rng), own(rng), noise(rng); b, y = bins(p, w)
    n = 2 * np.argsort(rng.random((N, 8, N * KC // 2)), axis=-1)[..., :R + 1]
    shine(rng, s, b, y, n[..., 1:], 5, 9); shine(rng, s, b, y, n[..., :1], 12, 15)
    return pack(s, p, w)
def setup_inputs_twins(rng):
    p, w, s, n = peps(rng), own(rng), noise(rng), np.zeros((N, 8, 1), np.int64)
    for r in range(N):
        for g in range(8):
            q, k = [int(v) for v in rng.permutation(N)[:2]]; i, j = sorted([KC * q + int(rng.integers(KC)), KC * k + int(rng.integers(KC))])
            if g == 0: i, j = 0, N * KC - 1
            if g == 1: i = KC * q + int(rng.integers(KC - 1)); j = i + 1; w[r, g, q, j % KC] = w[r, g, q, i % KC]
            if g == 2: i, j = KC - 1, KC
            p[j // KC, g, w[r, g, j // KC, j % KC]] = p[i // KC, g, w[r, g, i // KC, i % KC]]; n[r, g, 0] = i
    b, y = bins(p, w); shine(rng, s, b, y, some(rng), 5, 9); shine(rng, s, b, y, n, 15, 15)
    s[:, 3] = rng.integers(1, 16, (N, 16, 1)); return pack(s, p, w)
def setup_inputs_ends(rng):
    p, w, s, n = peps(rng), wants(rng), noise(rng), np.zeros((N, 8, 1), np.int64)
    p[0, :, 0] = LO; p[N - 1, :, V - 1] = HI; p[:, :, 1] = 64; p[:, :, 2] = HI; p[:, :, 2, 0] = LO
    w[..., 0] = 0; w[..., 1] = 1; w[..., 2] = 2; w[..., KC - 1] = V - 1
    n[:, 0::4] = 1; n[:, 1::4] = 0; n[:, 2::4] = N * KC - 1; n[:, 3::4] = 2
    b, y = bins(p, w); shine(rng, s, b, y, some(rng), 5, 9); shine(rng, s, b, y, n, 15, 15)
    s[..., 0] = 15; s[..., W - 1] = 15; return pack(s, p, w)
def setup_inputs_dark(rng):
    p, w, s = peps(rng), own(rng), noise(rng)
    for r in range(N):
        for g in range(8): p[0, g, w[r, g, 0, 0], 0] = LO
    b, y = bins(p, w); shine(rng, s, b, y, some(rng), 4, 15)
    for r in range(N):
        d = rng.permutation(8)
        for g in d[:3]: s[r, g][:, y[r, g].reshape(-1)] = 0; s[r, g][:, LO] = rng.integers(1, 16, 16)
        s[r, d[3]] = 0
        g = d[4]; t = int(rng.integers(1, N * KC)); s[r, g][:, y[r, g].reshape(-1)] = 0
        s[r, g][:, b[r, g, t]] = rng.integers(8, 16, (16, 16)); s[r, g][:, y[r, g, t]] = rng.integers(8, 16, (16, 16))
    return pack(s, p, w)
def setup_inputs_spread(rng):
    p = np.minimum(HI, LO + ((HI - LO + 1) * rng.random((N, 8, V, 16)) ** 3).astype(np.int64)); k = (N, 8, 1, W)
    s = (rng.integers(0, 16, (N, 8, 16, W)) >> rng.integers(0, 3, k)) * (rng.random(k) > 0.0625)
    return pack(s, p, wants(rng))
def check_inputs(d):
    bad = []; s = d["spec"].astype(np.float32); p = d["pep"].astype(np.float32); w = d["want"]
    if not ((s >= 0) & (s <= 15) & (s == np.floor(s))).all(): bad.append("spec")
    if not ((p >= LO) & (p <= HI) & (p == np.floor(p))).all(): bad.append("pep")
    if not ((w >= 0) & (w < V)).all(): bad.append("want")
    return bad
def reference(spec, pep, want):
    left = spec.astype(np.float32).reshape(N, 8, 16, W); m_ = pep.astype(np.float32).astype(np.int64).reshape(N, 8, 16, V)
    win = np.zeros((N, 8, R), np.float32); score = np.zeros((N, 8, R), np.float32)
    for r in range(N):
        e = gentries(want[r]).reshape(8, N, KC)
        for g in range(8):
            m = np.concatenate([m_[q, g][:, e[g, q]] for q in range(N)], axis=1)
            b = np.add.accumulate(m, axis=0); y = b[15] + 64 - b
            s = left[r, g]
            for t in range(R):
                sc = np.sum(s[:, b] * s[:, y], axis=(0, 1))
                n = int(np.argmax(sc)); win[r, g, t] = n; score[r, g, t] = sc[n]
                s[:, b[:, n]] = 0; s[:, y[:, n]] = 0
    return {"win": win, "score": score, "left": left.reshape(N, 128, W).astype(BF)}

@@ -1,0 +1,225 @@
+from concourse.bass import DstId, RemoteDMATransfer
+from concourse.mybir import AluOpType, AxisListType, ActivationFunctionType
+
+N, KC, W, V, R = 4, 64, 4096, 2048, 3
+F = 288
+YO = 64
+FIRST = [(0, 16, True), (16, 32, False), (32, 64, False)]
+LATER = [(0, 32, False), (32, 64, False)]
+
+SCRATCH = {
+    "wi": ("sbuf", [128, 16], "int32"),
+    "wl": ("sbuf", [128, 16], "uint16"),
+    "pepw": ("sbuf", [128, V], "bfloat16"),
+    "sw": ("sbuf", [128, W], "bfloat16"),
+    "ones": ("sbuf", [128, 128], "bfloat16"),
+    "blk": ("sbuf", [128, 128], "bfloat16"),
+    "lb": ("sbuf", [128, 128], "bfloat16"),
+    "ly": ("sbuf", [128, 128], "bfloat16"),
+    "wf": ("sbuf", [128, 128], "bfloat16"),
+    "idx": ("sbuf", [128, 256], "bfloat16"),
+    "zer": ("sbuf", [128, 16], "bfloat16"),
+    "pg": ("sbuf", [128, 256], "bfloat16"),
+    "yg": ("sbuf", [128, W], "bfloat16"),
+    "pr": ("sbuf", [128, W], "bfloat16"),
+    "tab": ("sbuf", [128, 512], "float32"),
+    "nk": ("sbuf", [128, 4], "float32"),
+    "hi": ("sbuf", [128, 4], "int32"),
+    "co": ("sbuf", [128, 8], "uint16"),
+    "wb": ("sbuf", [128, 16], "uint16"),
+    "wy": ("sbuf", [128, 16], "uint16"),
+    "winf": ("sbuf", [128, 4], "float32"),
+    "scf": ("sbuf", [128, 4], "float32"),
+    "key": ("psum", [128, 512], "float32"),
+}
+for _q in range(N):
+    SCRATCH["lst%d" % _q] = ("sbuf", [128, 16], "uint16")
+    SCRATCH["off%d" % _q] = ("sbuf", [128, 128], "uint16")
+    SCRATCH["rep%d" % _q] = ("sbuf", [128, 128], "uint16")
+    SCRATCH["ps%d" % _q] = ("psum", [128, 512], "float32")
+
+SEMAPHORES = (["ldw", "ldp", "lds", "conv", "vone", "vzer", "gb1", "gb2", "glb", "gix", "vly", "swf", "go", "lsent",
+               "rsent", "offr", "tabs", "yd", "pk", "red", "hs", "cs", "ws", "k1", "k2", "fin", "stl", "sts"]
+              + ["lst%d" % q for q in range(N)] + ["rp%d" % q for q in range(N)]
+              + ["pg%d" % q for q in range(N)] + ["po%d" % q for q in range(N)]
+              + ["rc%d" % q for q in range(N)] + ["pb%d" % q for q in range(N)]
+              + ["y%d" % k for k in range(10)])
+
+
+def rank_program(g, core, T, topo):
+    rank = T.rank_of(core)
+    if rank is None:
+        return
+    S = T.sem
+    v, act, pe, sp = g.vector, g.scalar, g.tensor, g.sync
+    op = AluOpType
+    copy = ActivationFunctionType.Copy
+    cores = T.cores
+
+    def far(q):
+        return 0 if topo.same_plane(topo.chip(cores[q]), topo.chip(core)) else 1
+
+    others = [q for q in range(N) if q != rank]
+    sends = sorted(others, key=lambda q: (far(q), (q - rank) % N))
+    order = [rank] + sorted(others, key=lambda q: (far(q), (rank - q) % N))
+    nin = {q: len(topo.engines(cores[q], core)) for q in others}
+    mask = topo.mask(core, cores[others[0]])
+    for q in others:
+        mask &= topo.mask(core, cores[q])
+    nall = len([e for e in topo.engines(core, cores[others[0]]) if mask >> e & 1])
+
+    off = [T["off%d" % q] for q in range(N)]
+    ps = [T["ps%d" % q] for q in range(N)]
+
+    pieces = []
+    for b, q in enumerate(order):
+        for (a, z, mine) in (FIRST if b == 0 else LATER):
+            pieces.append((b, q, a, z, mine, len(pieces)))
+    count = [len([p for p in pieces if p[0] == b]) for b in range(N)]
+
+    sp.dma_start(T.wi[:], T.want[:]).then_inc(S.ldw, 16)
+    sp.dma_start(T.pepw[:], T.pep[:]).then_inc(S.ldp, 16)
+    sp.wait_ge(S.go, 1)
+    sp.dma_start(T.sw[:], T.spec[:]).then_inc(S.lds, 16)
+
+    g.wait_ge(S.vone, 1)
+    g.affine_select(T.blk[:], T.ones[:], [[-16, 8], [0, 16]], op.is_ge, 0.0, 0, 1).then_inc(S.gb1, 1)
+    g.wait_ge(S.gb1, 1)
+    g.affine_select(T.blk[:], T.blk[:], [[16, 8], [0, 16]], op.is_ge, 0.0, 15, -1).then_inc(S.gb2, 1)
+    g.wait_ge(S.gb2, 1)
+    g.affine_select(T.lb[:], T.blk[:], [[1, 128]], op.is_ge, 0.0, 0, -1).then_inc(S.glb, 1)
+    g.wait_ge(S.conv, 1)
+    ids = []
+    for q in sends:
+        rid, pid, _ = topo.addr(cores[q])
+        ids.append(DstId(rid=rid, pnc=pid))
+    land = T["lst%d" % rank]
+    g.remote_dma_fused([RemoteDMATransfer(dst_ids=ids, dma_engine_mask=mask, remote_sem=S["lst%d" % rank],
+                                          srcs=[T.wl[:]], dsts=[land[:] for q in sends])], local_sem=S.lsent)
+    g.sem_inc(S.go, 1)
+    g.iota(T.idx[0:1, 0:256], [[-1, 256]], 0, 0, allow_small_or_imprecise_dtypes=True).then_inc(S.gix, 1)
+    total = 0
+    for q in sends:
+        g.wait_ge(S["rc%d" % q], 1)
+        rid, pid, _ = topo.addr(cores[q])
+        g.remote_dma(off[rank][:], T["rep%d" % q][:], S["rp%d" % rank], S.rsent, pid, rid, topo.mask(core, cores[q]))
+        total += len(topo.engines(core, cores[q]))
+
+    def bins_mm(q, slot):
+        pe.wait_ge(S["pg%d" % q], 1)
+        G = T.pg[:, KC * slot:KC * slot + KC]
+        pe.matmul(ps[q][:, 0:KC], T.lb[:], G, True, True)
+        pe.matmul(ps[q][:, KC:2 * KC], T.ly[:], G, True, True).then_inc(S["po%d" % q], 1)
+
+    pe.wait_ge(S.glb, 1)
+    pe.wait_ge(S.vly, 1)
+    bins_mm(rank, 0)
+    for s, q in enumerate(sends):
+        bins_mm(q, s + 1)
+    pe.wait_ge(S.swf, 1)
+    pe.wait_ge(S.gix, 1)
+    for t in range(R):
+        if t:
+            pe.wait_ge(S.red, t)
+        for b, q in enumerate(order):
+            dst = T.key[:, KC * q:KC * q + KC]
+            pe.matmul(dst, T.ones[0:1, 0:128], T.idx[0:1, KC * q:KC * q + KC], True, False)
+            pe.wait_ge(S["pb%d" % b], count[b] * (t + 1))
+            for i in range(16):
+                mm = pe.matmul(dst, T.wf[:], T.pr[:, 1024 * b + i:1024 * (b + 1):16], False, i == 15)
+            mm.then_inc(S.pk, 1)
+
+    act.wait_ge(S.gb2, 1)
+    act.activation(T.wf[:], T.blk[:], copy, scale=float(F)).then_inc(S.swf, 1)
+    for t in range(R):
+        seen = []
+        if t == 0:
+            act.wait_ge(S.lds, 16)
+        else:
+            act.wait_ge(S.k2, t)
+        for (b, q, a, z, mine, k) in pieces:
+            if mine:
+                continue
+            if t == 0 and q not in seen:
+                seen.append(q)
+                if q == rank:
+                    act.wait_ge(S.offr, 1)
+                else:
+                    act.wait_ge(S["rp%d" % q], nin[q])
+            act.activation(T.yg[:, 1024 * b + 16 * a:1024 * b + 16 * z],
+                           T.sw[:, YO:W].indirect(off[q][:, KC + a:KC + z]), copy).then_inc(S["y%d" % k], 1)
+
+    v.memset(T.ones[:], 1.0).then_inc(S.vone, 1)
+    v.memset(T.zer[:], 0.0).then_inc(S.vzer, 1)
+    v.wait_ge(S.ldw, 16)
+    v.tensor_copy(T.wl[:], T.wi[:]).then_inc(S.conv, 1)
+    v.wait_ge(S.conv, 1)
+    v.wait_ge(S.ldp, 16)
+    v.tensor_copy(T.pg[:, 0:KC], T.pepw[:].indirect(T.wl[:, 4 * rank:4 * rank + 4])).then_inc(S["pg%d" % rank], 1)
+    v.wait_ge(S.glb, 1)
+    v.tensor_tensor(T.ly[:], T.blk[:], T.lb[:], op.subtract).then_inc(S.vly, 1)
+    v.wait_ge(S["po%d" % rank], 1)
+    v.tensor_copy(off[rank][:], ps[rank][:, 0:2 * KC]).then_inc(S.offr, 1)
+
+    def pick(q, slot):
+        v.wait_ge(S["lst%d" % q], nin[q])
+        v.tensor_copy(T.pg[:, KC * slot:KC * slot + KC],
+                      T.pepw[:].indirect(T["lst%d" % q][:, 4 * rank:4 * rank + 4])).then_inc(S["pg%d" % q], 1)
+
+    def pack(q):
+        v.wait_ge(S["po%d" % q], 1)
+        v.tensor_copy(T["rep%d" % q][:], ps[q][:, 0:2 * KC]).then_inc(S["rc%d" % q], 1)
+
+    pick(sends[0], 1)
+    pack(sends[0])
+    pick(sends[1], 2)
+    pick(sends[2], 3)
+    pack(sends[1])
+    pack(sends[2])
+    v.wait_ge(S.offr, 1)
+    v.wait_ge(S.lds, 16)
+    v.wait_ge(S.vzer, 1)
+    for t in range(R):
+        for (b, q, a, z, mine, k) in pieces:
+            y = T.yg[:, 1024 * b + 16 * a:1024 * b + 16 * z]
+            if mine:
+                v.tensor_copy(y, T.sw[:, YO:W].indirect(off[q][:, KC + a:KC + z])).then_inc(S.yd, 1)
+                v.wait_ge(S.yd, t + 1)
+            else:
+                v.wait_ge(S["y%d" % k], t + 1)
+            v.tensor_tensor(T.pr[:, 1024 * b + 16 * a:1024 * b + 16 * z], T.sw[:].indirect(off[q][:, a:z]), y,
+                            op.mult).then_inc(S["pb%d" % b], 1)
+        if t == 0:
+            for q in range(N):
+                v.tensor_copy(T.tab[:, KC * q:KC * q + KC], off[q][:, 0:KC]).then_inc(S.tabs, 1)
+                v.tensor_copy(T.tab[:, 256 + KC * q:256 + KC * q + KC], off[q][:, KC:2 * KC]).then_inc(S.tabs, 1)
+            v.wait_ge(S.tabs, 2 * N)
+        v.wait_ge(S.pk, N * (t + 1))
+        v.tensor_reduce(T.nk[:, t:t + 1], T.key[:, 0:256], AxisListType.X, op.max, negate=True).then_inc(S.red, 1)
+        v.wait_ge(S.red, t + 1)
+        v.tensor_scalar(T.hi[:, t:t + 1], T.nk[:, t:t + 1], -128.0, 1.0 / F, op.add, op.mult).then_inc(S.hs, 1)
+        v.wait_ge(S.hs, t + 1)
+        v.tensor_scalar(T.co[:, 2 * t:2 * t + 1], T.hi[:, t:t + 1], -float(F), T.nk[:, t:t + 1],
+                        op.mult, op.add).then_inc(S.cs, 1)
+        v.wait_ge(S.cs, t + 1)
+        pos = T.co[:, 2 * t:2 * t + 1]
+        v.tensor_copy(T.wb[:], T.tab[:, 0:256].indirect(pos)).then_inc(S.ws, 1)
+        v.tensor_copy(T.wy[:], T.tab[:, 256:512].indirect(pos)).then_inc(S.ws, 1)
+        v.wait_ge(S.ws, 2 * (t + 1))
+        v.tensor_copy(T.sw[:].indirect(T.wb[:, 0:1]), T.zer[:]).then_inc(S.k1, 1)
+        v.wait_ge(S.k1, t + 1)
+        v.tensor_copy(T.sw[:, YO:W].indirect(T.wy[:, 0:1]), T.zer[:]).then_inc(S.k2, 1)
+        if t < R - 1:
+            v.wait_ge(S.k2, t + 1)
+    v.tensor_copy(T.winf[:, 0:R], T.co[:, 0:2 * R:2]).then_inc(S.fin, 1)
+    v.tensor_scalar(T.scf[:, 0:R], T.hi[:, 0:R], -1.0, None, op.mult).then_inc(S.fin, 1)
+
+    sp.wait_ge(S.k2, R)
+    sp.dma_start(T.left[:], T.sw[:]).then_inc(S.stl, 16)
+    act.wait_ge(S.fin, 2)
+    act.dma_start(T.win[:], T.winf[0:128:16, 0:R]).then_inc(S.sts, 16)
+    act.dma_start(T.score[:], T.scf[0:128:16, 0:R]).then_inc(S.sts, 16)
+    sp.wait_ge(S.stl, 16)
+    act.wait_ge(S.sts, 32)
+    g.wait_ge(S.lsent, nall)
+    g.wait_ge(S.rsent, total)

@@ -4,46 +4,53 @@ from concourse.mybir import AluOpType, AxisListType, ActivationFunctionType
 N, KC, W, V, R = 4, 64, 4096, 2048, 3
 F = 288
 YO = 64
-FIRST = [(0, 16, True), (16, 32, False), (32, 64, False)]
-LATER = [(0, 32, False), (32, 64, False)]
+H = 64
+PC = 32
+BL = 16 * PC
+CUTS = [0, 16, 32, 42, 52, 64, 74, 84, 96, 128]
+MINE = 8
 
 SCRATCH = {
     "wi": ("sbuf", [128, 16], "int32"),
     "wl": ("sbuf", [128, 16], "uint16"),
     "pepw": ("sbuf", [128, V], "bfloat16"),
-    "sw": ("sbuf", [128, W], "bfloat16"),
+    "mas": ("sbuf", [128, N * KC], "bfloat16"),
+    "pn": ("sbuf", [128, 1], "int32"),
+    "pi": ("sbuf", [128, 4], "int32"),
+    "pc": ("sbuf", [128, 4], "bfloat16"),
+    "sp": ("sbuf", [128, 1], "float32"),
     "ones": ("sbuf", [128, 128], "bfloat16"),
-    "blk": ("sbuf", [128, 128], "bfloat16"),
-    "lb": ("sbuf", [128, 128], "bfloat16"),
-    "ly": ("sbuf", [128, 128], "bfloat16"),
-    "wf": ("sbuf", [128, 128], "bfloat16"),
     "idx": ("sbuf", [128, 256], "bfloat16"),
     "zer": ("sbuf", [128, 16], "bfloat16"),
-    "pg": ("sbuf", [128, 256], "bfloat16"),
-    "yg": ("sbuf", [128, W], "bfloat16"),
-    "pr": ("sbuf", [128, W], "bfloat16"),
-    "tab": ("sbuf", [128, 512], "float32"),
-    "nk": ("sbuf", [128, 4], "float32"),
-    "hi": ("sbuf", [128, 4], "int32"),
-    "co": ("sbuf", [128, 8], "uint16"),
-    "wb": ("sbuf", [128, 16], "uint16"),
-    "wy": ("sbuf", [128, 16], "uint16"),
+    "nk": ("sbuf", [128, 8], "float32"),
+    "hi": ("sbuf", [128, 8], "int32"),
+    "co": ("sbuf", [128, 16], "uint16"),
     "winf": ("sbuf", [128, 4], "float32"),
     "scf": ("sbuf", [128, 4], "float32"),
-    "key": ("psum", [128, 512], "float32"),
+    "pa0": ("psum", [128, 512], "float32"),
+    "pa1": ("psum", [128, 512], "float32"),
+    "pb": ("psum", [128, 512], "float32"),
 }
+for _n in ("los", "th", "im", "tb", "tn", "e0", "e1", "mb0", "mb1", "my0", "my1", "blk", "nb", "ny", "wf"):
+    SCRATCH[_n] = ("sbuf", [128, 128], "bfloat16")
+for _x in range(2):
+    SCRATCH["sw%d" % _x] = ("sbuf", [128, W], "bfloat16")
+    SCRATCH["yg%d" % _x] = ("sbuf", [128, N * BL], "bfloat16")
+    SCRATCH["pr%d" % _x] = ("sbuf", [128, N * BL], "bfloat16")
+    SCRATCH["off%d" % _x] = ("sbuf", [128, 2 * PC * N], "uint16")
+    SCRATCH["tab%d" % _x] = ("sbuf", [128, F + 256], "float32")
+    SCRATCH["wb%d" % _x] = ("sbuf", [128, 16], "uint16")
+    SCRATCH["key%d" % _x] = ("psum", [128, 512], "float32")
+    SCRATCH["tp%d" % _x] = ("psum", [128, 512], "float32")
 for _q in range(N):
     SCRATCH["lst%d" % _q] = ("sbuf", [128, 16], "uint16")
-    SCRATCH["off%d" % _q] = ("sbuf", [128, 128], "uint16")
-    SCRATCH["rep%d" % _q] = ("sbuf", [128, 128], "uint16")
-    SCRATCH["ps%d" % _q] = ("psum", [128, 512], "float32")
+    SCRATCH["rep%d" % _q] = ("sbuf", [128, KC], "bfloat16")
 
-SEMAPHORES = (["ldw", "ldp", "lds", "conv", "vone", "vzer", "gb1", "gb2", "glb", "gix", "vly", "swf", "go", "lsent",
-               "rsent", "offr", "tabs", "yd", "pk", "red", "hs", "cs", "ws", "k1", "k2", "fin", "stl", "sts"]
-              + ["lst%d" % q for q in range(N)] + ["rp%d" % q for q in range(N)]
-              + ["pg%d" % q for q in range(N)] + ["po%d" % q for q in range(N)]
-              + ["rc%d" % q for q in range(N)] + ["pb%d" % q for q in range(N)]
-              + ["y%d" % k for k in range(10)])
+SEMAPHORES = (["ldw", "ldp", "conv", "vone", "vzer", "g1", "g2", "g3", "g4", "gix", "c1", "c2", "c3", "m1", "m2", "m3",
+               "m4", "m5", "m6", "swf", "go", "go2", "lsent", "rsent", "yd", "fin", "stl", "sts", "pob", "pab"]
+              + [n + str(x) for x in range(2) for n in ("lds", "tm", "tabs", "pk", "red", "hs", "cs", "ws", "ka", "kb", "yf")]
+              + [n + str(q) for q in range(N) for n in ("lst", "rp", "pg", "po", "pa")]
+              + [n + str(x) + str(b) for x in range(2) for b in range(N) for n in ("y", "pb")])
 
 
 def rank_program(g, core, T, topo):
@@ -68,158 +75,253 @@ def rank_program(g, core, T, topo):
         mask &= topo.mask(core, cores[q])
     nall = len([e for e in topo.engines(core, cores[others[0]]) if mask >> e & 1])
 
-    off = [T["off%d" % q] for q in range(N)]
-    ps = [T["ps%d" % q] for q in range(N)]
+    sw, yg, pr, off = [T.sw0, T.sw1], [T.yg0, T.yg1], [T.pr0, T.pr1], [T.off0, T.off1]
+    tab, wb, key, tp = [T.tab0, T.tab1], [T.wb0, T.wb1], [T.key0, T.key1], [T.tp0, T.tp1]
+    pa = [T.pa0, T.pa1]
+    half = [slice(0, H), slice(H, 2 * H)]
+    phases = [(x, t) for t in range(R) for x in range(2)]
 
-    pieces = []
-    for b, q in enumerate(order):
-        for (a, z, mine) in (FIRST if b == 0 else LATER):
-            pieces.append((b, q, a, z, mine, len(pieces)))
-    count = [len([p for p in pieces if p[0] == b]) for b in range(N)]
+    def s2(name, *k):
+        return S[name + "".join(str(i) for i in k)]
 
     sp.dma_start(T.wi[:], T.want[:]).then_inc(S.ldw, 16)
     sp.dma_start(T.pepw[:], T.pep[:]).then_inc(S.ldp, 16)
-    sp.wait_ge(S.go, 1)
-    sp.dma_start(T.sw[:], T.spec[:]).then_inc(S.lds, 16)
+    for x, gate in ((0, S.go), (1, S.go2)):
+        sp.wait_ge(gate, 1)
+        for h in range(2):
+            sp.dma_start(sw[x][half[h], :], T.spec[half[x], :]).then_inc(s2("lds", x), 16)
 
-    g.wait_ge(S.vone, 1)
-    g.affine_select(T.blk[:], T.ones[:], [[-16, 8], [0, 16]], op.is_ge, 0.0, 0, 1).then_inc(S.gb1, 1)
-    g.wait_ge(S.gb1, 1)
-    g.affine_select(T.blk[:], T.blk[:], [[16, 8], [0, 16]], op.is_ge, 0.0, 15, -1).then_inc(S.gb2, 1)
-    g.wait_ge(S.gb2, 1)
-    g.affine_select(T.lb[:], T.blk[:], [[1, 128]], op.is_ge, 0.0, 0, -1).then_inc(S.glb, 1)
+    g.iota(T.pn[:], [[0, 1]], 0, 1).then_inc(S.g1, 1)
+    g.iota(T.los[:], [[0, 2], [1, 8], [0, 8]], 0, 0, allow_small_or_imprecise_dtypes=True).then_inc(S.g2, 1)
+    g.iota(T.th[:], [[8, 2], [0, 8], [1, 8]], 0, 0, allow_small_or_imprecise_dtypes=True).then_inc(S.g3, 1)
     g.wait_ge(S.conv, 1)
     ids = []
     for q in sends:
         rid, pid, _ = topo.addr(cores[q])
         ids.append(DstId(rid=rid, pnc=pid))
     land = T["lst%d" % rank]
-    g.remote_dma_fused([RemoteDMATransfer(dst_ids=ids, dma_engine_mask=mask, remote_sem=S["lst%d" % rank],
+    g.remote_dma_fused([RemoteDMATransfer(dst_ids=ids, dma_engine_mask=mask, remote_sem=s2("lst", rank),
                                           srcs=[T.wl[:]], dsts=[land[:] for q in sends])], local_sem=S.lsent)
     g.sem_inc(S.go, 1)
-    g.iota(T.idx[0:1, 0:256], [[-1, 256]], 0, 0, allow_small_or_imprecise_dtypes=True).then_inc(S.gix, 1)
+    g.iota(T.im[:], [[0, 8], [1, 16]], 0, 0, allow_small_or_imprecise_dtypes=True).then_inc(S.g4, 1)
     total = 0
     for q in sends:
-        g.wait_ge(S["rc%d" % q], 1)
+        g.wait_ge(s2("pg", q), 1)
         rid, pid, _ = topo.addr(cores[q])
-        g.remote_dma(off[rank][:], T["rep%d" % q][:], S["rp%d" % rank], S.rsent, pid, rid, topo.mask(core, cores[q]))
+        g.remote_dma(T.mas[:, KC * rank:KC * rank + KC], T["rep%d" % q][:], s2("rp", rank), S.rsent, pid, rid,
+                     topo.mask(core, cores[q]))
         total += len(topo.engines(core, cores[q]))
+    g.sem_inc(S.go2, 1)
+    g.iota(T.idx[0:1, 0:256], [[-1, 256]], 0, 0, allow_small_or_imprecise_dtypes=True).then_inc(S.gix, 1)
 
-    def bins_mm(q, slot):
-        pe.wait_ge(S["pg%d" % q], 1)
-        G = T.pg[:, KC * slot:KC * slot + KC]
-        pe.matmul(ps[q][:, 0:KC], T.lb[:], G, True, True)
-        pe.matmul(ps[q][:, KC:2 * KC], T.ly[:], G, True, True).then_inc(S["po%d" % q], 1)
+    def bins_mm(x, b, bank):
+        q, c = order[b], 2 * PC * b
+        for w, mats in enumerate(((T.mb0, T.mb1), (T.my0, T.my1))):
+            for s in range(2):
+                mm = pe.matmul(bank[:, c + PC * w:c + PC * w + PC], mats[s][half[x], :],
+                               T.mas[half[x], KC * q + s:KC * q + KC:2], s == 0, s == 1)
+        return mm
 
-    pe.wait_ge(S.glb, 1)
-    pe.wait_ge(S.vly, 1)
-    bins_mm(rank, 0)
-    for s, q in enumerate(sends):
-        bins_mm(q, s + 1)
+    def tab_mm(x):
+        pe.matmul(tp[x][:, 0:256], T.nb[half[x], :], T.mas[half[x], :], True, True)
+        pe.matmul(tp[x][:, 256:512], T.ny[half[x], :], T.mas[half[x], :], True, True).then_inc(s2("tm", x), 1)
+
+    pe.wait_ge(S.m3, 2)
+    for b, q in enumerate(order):
+        pe.wait_ge(s2("rp" if b else "pg", q), nin[q] if b else 1)
+        if b >= 2:
+            pe.wait_ge(s2("pa", b - 2), 1)
+        bins_mm(0, b, pa[b % 2]).then_inc(s2("po", b), 1)
+        mm = bins_mm(1, b, T.pb)
+    mm.then_inc(S.pob, 1)
     pe.wait_ge(S.swf, 1)
     pe.wait_ge(S.gix, 1)
-    for t in range(R):
+    pe.wait_ge(S.vone, 1)
+    pe.wait_ge(S.m6, 1)
+    done = {}
+    for n, (x, t) in enumerate(phases):
         if t:
-            pe.wait_ge(S.red, t)
+            pe.wait_ge(s2("red", x), t)
         for b, q in enumerate(order):
-            dst = T.key[:, KC * q:KC * q + KC]
+            dst = key[x][:, KC * q:KC * q + KC]
             pe.matmul(dst, T.ones[0:1, 0:128], T.idx[0:1, KC * q:KC * q + KC], True, False)
-            pe.wait_ge(S["pb%d" % b], count[b] * (t + 1))
-            for i in range(16):
-                mm = pe.matmul(dst, T.wf[:], T.pr[:, 1024 * b + i:1024 * (b + 1):16], False, i == 15)
-            mm.then_inc(S.pk, 1)
+            cuts = [c for c in CUTS[:-1] if c // PC == b]
+            done[x, b] = done.get((x, b), 0) + (len(cuts) if n else 1 if b else 2)
+            pe.wait_ge(s2("pb", x, b), done[x, b])
+            for i in range(8):
+                mm = pe.matmul(dst, T.wf[:], pr[x][:, BL * b + i:BL * (b + 1):8], False, i == 7)
+            mm.then_inc(s2("pk", x), 1)
+            if n == 0 and b == 1:
+                tab_mm(0)
+            if n == 1 and b == 0:
+                tab_mm(1)
 
-    act.wait_ge(S.gb2, 1)
+    def ygather(x, b, a, z, sem):
+        c = 2 * PC * b + PC
+        act.activation(yg[x][:, BL * b + 16 * a:BL * b + 16 * z],
+                       sw[x][:, YO:W].indirect(off[x][:, c + a:c + z]), copy).then_inc(sem, 1)
+
+    act.wait_ge(S.m4, 1)
     act.activation(T.wf[:], T.blk[:], copy, scale=float(F)).then_inc(S.swf, 1)
-    for t in range(R):
-        seen = []
+    for n, (x, t) in enumerate(phases):
         if t == 0:
-            act.wait_ge(S.lds, 16)
+            act.wait_ge(s2("lds", x), 32)
         else:
-            act.wait_ge(S.k2, t)
-        for (b, q, a, z, mine, k) in pieces:
-            if mine:
-                continue
-            if t == 0 and q not in seen:
-                seen.append(q)
-                if q == rank:
-                    act.wait_ge(S.offr, 1)
-                else:
-                    act.wait_ge(S["rp%d" % q], nin[q])
-            act.activation(T.yg[:, 1024 * b + 16 * a:1024 * b + 16 * z],
-                           T.sw[:, YO:W].indirect(off[q][:, KC + a:KC + z]), copy).then_inc(S["y%d" % k], 1)
+            act.wait_ge(s2("kb", x), t)
+        if n == 1:
+            act.wait_ge(S.pab, 1)
+        for b in range(N):
+            if n == 0:
+                act.wait_ge(s2("pa", b), 1)
+                ygather(x, b, 0 if b else MINE, PC, s2("y", x, b))
+            elif b == 0:
+                ygather(x, b, 0, PC // 2, s2("yf", x))
+                ygather(x, b, PC // 2, PC, s2("y", x, b))
+            else:
+                ygather(x, b, 0, PC, s2("y", x, b))
+            if n in (1, 2) and b == 1:
+                o = 1 - x
+                act.wait_ge(s2("tm", o), 1)
+                act.activation(tab[o][:, 0:256], tp[o][:, 0:256], copy).then_inc(s2("tabs", o), 1)
+                act.activation(tab[o][:, F:F + 256], tp[o][:, 256:512], copy).then_inc(s2("tabs", o), 1)
 
-    v.memset(T.ones[:], 1.0).then_inc(S.vone, 1)
+    v.wait_ge(S.g1, 1)
+    v.tensor_scalar(T.pi[:, 0:1], T.pn[:], 15, None, op.bitwise_and).then_inc(S.c1, 1)
+    v.tensor_scalar(T.pi[:, 1:2], T.pn[:], 3, 6, op.logical_shift_right, op.bitwise_and).then_inc(S.c1, 1)
+    v.tensor_scalar(T.pi[:, 2:3], T.pn[:], 8, None, op.bitwise_and).then_inc(S.c1, 1)
+    v.memset(T.ones[0:1, :], 1.0).then_inc(S.vone, 1)
     v.memset(T.zer[:], 0.0).then_inc(S.vzer, 1)
+    v.wait_ge(S.c1, 3)
+    v.tensor_copy(T.pc[:, 0:2], T.pi[:, 0:2]).then_inc(S.c2, 1)
+    v.tensor_scalar(T.sp[:], T.pi[:, 2:3], -F / 8.0, -128.0, op.mult, op.add).then_inc(S.c3, 1)
+    for x in range(2):
+        v.memset(tab[x][:, 256:F], 0.0).then_inc(S.vzer, 1)
+    v.wait_ge(S.c2, 1)
+    row, two = T.pc[:, 0:1], T.pc[:, 1:2]
+    v.wait_ge(S.g2, 1)
+    v.tensor_scalar(T.e0[:], T.los[:], two, None, op.is_equal).then_inc(S.m1, 1)
+    v.tensor_scalar(T.e1[:], T.los[:], -1.0, two, op.add, op.is_equal).then_inc(S.m1, 1)
+    v.wait_ge(S.g3, 1)
+    v.tensor_scalar(T.tb[:], T.th[:], row, None, op.is_ge).then_inc(S.m1, 1)
     v.wait_ge(S.ldw, 16)
     v.tensor_copy(T.wl[:], T.wi[:]).then_inc(S.conv, 1)
+    v.wait_ge(S.m1, 3)
+    v.tensor_tensor(T.mb0[:], T.tb[:], T.e0[:], op.mult).then_inc(S.m2, 1)
+    v.tensor_tensor(T.mb1[:], T.tb[:], T.e1[:], op.mult).then_inc(S.m2, 1)
+    v.tensor_tensor(T.blk[:], T.e0[:], T.e1[:], op.add).then_inc(S.m4, 1)
+    v.wait_ge(S.m2, 2)
+    v.tensor_tensor(T.my0[:], T.e0[:], T.mb0[:], op.subtract).then_inc(S.m3, 1)
+    v.tensor_tensor(T.my1[:], T.e1[:], T.mb1[:], op.subtract).then_inc(S.m3, 1)
     v.wait_ge(S.conv, 1)
     v.wait_ge(S.ldp, 16)
-    v.tensor_copy(T.pg[:, 0:KC], T.pepw[:].indirect(T.wl[:, 4 * rank:4 * rank + 4])).then_inc(S["pg%d" % rank], 1)
-    v.wait_ge(S.glb, 1)
-    v.tensor_tensor(T.ly[:], T.blk[:], T.lb[:], op.subtract).then_inc(S.vly, 1)
-    v.wait_ge(S["po%d" % rank], 1)
-    v.tensor_copy(off[rank][:], ps[rank][:, 0:2 * KC]).then_inc(S.offr, 1)
+    v.tensor_copy(T.mas[:, KC * rank:KC * rank + KC],
+                  T.pepw[:].indirect(T.wl[:, 4 * rank:4 * rank + 4])).then_inc(s2("pg", rank), 1)
+    v.wait_ge(S.g4, 1)
+    v.tensor_scalar(T.tn[:], T.im[:], row, None, op.is_ge).then_inc(S.m5, 1)
+    v.wait_ge(S.m4, 1)
+    v.wait_ge(S.m5, 1)
+    v.tensor_tensor(T.nb[:], T.tn[:], T.blk[:], op.mult).then_inc(S.m5, 1)
 
-    def pick(q, slot):
-        v.wait_ge(S["lst%d" % q], nin[q])
-        v.tensor_copy(T.pg[:, KC * slot:KC * slot + KC],
-                      T.pepw[:].indirect(T["lst%d" % q][:, 4 * rank:4 * rank + 4])).then_inc(S["pg%d" % q], 1)
+    def pack(b):
+        c = 2 * PC * b
+        v.wait_ge(s2("po", b), 1)
+        v.tensor_copy(off[0][:, c:c + 2 * PC], pa[b % 2][:, c:c + 2 * PC]).then_inc(s2("pa", b), 1)
 
-    def pack(q):
-        v.wait_ge(S["po%d" % q], 1)
-        v.tensor_copy(T["rep%d" % q][:], ps[q][:, 0:2 * KC]).then_inc(S["rc%d" % q], 1)
+    pack(0)
+    for q in sends:
+        v.wait_ge(s2("lst", q), nin[q])
+        v.tensor_copy(T["rep%d" % q][:],
+                      T.pepw[:].indirect(T["lst%d" % q][:, 4 * rank:4 * rank + 4])).then_inc(s2("pg", q), 1)
+    v.wait_ge(S.m5, 2)
+    v.tensor_tensor(T.ny[:], T.blk[:], T.nb[:], op.subtract).then_inc(S.m6, 1)
+    v.wait_ge(S.vzer, 3)
+    v.wait_ge(S.c3, 1)
 
-    pick(sends[0], 1)
-    pack(sends[0])
-    pick(sends[1], 2)
-    pick(sends[2], 3)
-    pack(sends[1])
-    pack(sends[2])
-    v.wait_ge(S.offr, 1)
-    v.wait_ge(S.lds, 16)
-    v.wait_ge(S.vzer, 1)
-    for t in range(R):
-        for (b, q, a, z, mine, k) in pieces:
-            y = T.yg[:, 1024 * b + 16 * a:1024 * b + 16 * z]
-            if mine:
-                v.tensor_copy(y, T.sw[:, YO:W].indirect(off[q][:, KC + a:KC + z])).then_inc(S.yd, 1)
-                v.wait_ge(S.yd, t + 1)
-            else:
-                v.wait_ge(S["y%d" % k], t + 1)
-            v.tensor_tensor(T.pr[:, 1024 * b + 16 * a:1024 * b + 16 * z], T.sw[:].indirect(off[q][:, a:z]), y,
-                            op.mult).then_inc(S["pb%d" % b], 1)
-        if t == 0:
-            for q in range(N):
-                v.tensor_copy(T.tab[:, KC * q:KC * q + KC], off[q][:, 0:KC]).then_inc(S.tabs, 1)
-                v.tensor_copy(T.tab[:, 256 + KC * q:256 + KC * q + KC], off[q][:, KC:2 * KC]).then_inc(S.tabs, 1)
-            v.wait_ge(S.tabs, 2 * N)
-        v.wait_ge(S.pk, N * (t + 1))
-        v.tensor_reduce(T.nk[:, t:t + 1], T.key[:, 0:256], AxisListType.X, op.max, negate=True).then_inc(S.red, 1)
-        v.wait_ge(S.red, t + 1)
-        v.tensor_scalar(T.hi[:, t:t + 1], T.nk[:, t:t + 1], -128.0, 1.0 / F, op.add, op.mult).then_inc(S.hs, 1)
-        v.wait_ge(S.hs, t + 1)
-        v.tensor_scalar(T.co[:, 2 * t:2 * t + 1], T.hi[:, t:t + 1], -float(F), T.nk[:, t:t + 1],
-                        op.mult, op.add).then_inc(S.cs, 1)
-        v.wait_ge(S.cs, t + 1)
-        pos = T.co[:, 2 * t:2 * t + 1]
-        v.tensor_copy(T.wb[:], T.tab[:, 0:256].indirect(pos)).then_inc(S.ws, 1)
-        v.tensor_copy(T.wy[:], T.tab[:, 256:512].indirect(pos)).then_inc(S.ws, 1)
-        v.wait_ge(S.ws, 2 * (t + 1))
-        v.tensor_copy(T.sw[:].indirect(T.wb[:, 0:1]), T.zer[:]).then_inc(S.k1, 1)
-        v.wait_ge(S.k1, t + 1)
-        v.tensor_copy(T.sw[:, YO:W].indirect(T.wy[:, 0:1]), T.zer[:]).then_inc(S.k2, 1)
-        if t < R - 1:
-            v.wait_ge(S.k2, t + 1)
-    v.tensor_copy(T.winf[:, 0:R], T.co[:, 0:2 * R:2]).then_inc(S.fin, 1)
-    v.tensor_scalar(T.scf[:, 0:R], T.hi[:, 0:R], -1.0, None, op.mult).then_inc(S.fin, 1)
+    def product(x, b, a, z):
+        c = 2 * PC * b
+        v.tensor_tensor(pr[x][:, BL * b + 16 * a:BL * b + 16 * z], sw[x][:].indirect(off[x][:, c + a:c + z]),
+                        yg[x][:, BL * b + 16 * a:BL * b + 16 * z], op.mult).then_inc(s2("pb", x, b), 1)
 
-    sp.wait_ge(S.k2, R)
-    sp.dma_start(T.left[:], T.sw[:]).then_inc(S.stl, 16)
-    act.wait_ge(S.fin, 2)
+    def end_steps(x, t):
+        k = R * x + t
+        nk, hi, co = T.nk[:, k:k + 1], T.hi[:, k:k + 1], T.co[:, 2 * k:2 * k + 1]
+
+        def best():
+            v.wait_ge(s2("pk", x), N * (t + 1))
+            v.tensor_reduce(nk, key[x][:, 0:256], AxisListType.X, op.max, negate=True).then_inc(s2("red", x), 1)
+
+        def score():
+            v.wait_ge(s2("red", x), t + 1)
+            v.tensor_scalar(hi, nk, T.sp[:], 1.0 / F, op.add, op.mult).then_inc(s2("hs", x), 1)
+
+        def place():
+            v.wait_ge(s2("hs", x), t + 1)
+            v.tensor_scalar(co, hi, -float(F), nk, op.mult, op.add).then_inc(s2("cs", x), 1)
+
+        def fetch():
+            v.wait_ge(s2("cs", x), t + 1)
+            if t == 0:
+                v.wait_ge(s2("tabs", x), 2)
+            v.tensor_copy(wb[x][:], tab[x][:].indirect(co)).then_inc(s2("ws", x), 1)
+
+        def erase_b():
+            v.wait_ge(s2("ws", x), t + 1)
+            v.tensor_copy(sw[x][:].indirect(wb[x][:, 0:1]), T.zer[:]).then_inc(s2("ka", x), 1)
+
+        def erase_y():
+            v.wait_ge(s2("ka", x), t + 1)
+            v.tensor_copy(sw[x][:, YO:W].indirect(wb[x][:, 8:9]), T.zer[:]).then_inc(s2("kb", x), 1)
+
+        return [best, score, place, fetch, erase_b, erase_y]
+
+    def results(x):
+        v.tensor_copy(T.winf[half[x], 0:R], T.co[half[x], 2 * R * x:2 * R * x + 2 * R:2]).then_inc(S.fin, 1)
+        v.tensor_scalar(T.scf[half[x], 0:R], T.hi[half[x], R * x:R * x + R], -1.0, None, op.mult).then_inc(S.fin, 1)
+
+    v.wait_ge(S.lds0, 32)
+    v.wait_ge(s2("pa", 0), 1)
+    v.tensor_copy(yg[0][:, 0:16 * MINE], sw[0][:, YO:W].indirect(off[0][:, PC:PC + MINE])).then_inc(S.yd, 1)
+    pack(1)
+    v.wait_ge(S.yd, 1)
+    product(0, 0, 0, MINE)
+    for b in range(N):
+        if 2 <= b + 1 < N:
+            pack(b + 1)
+        if b == 2:
+            v.wait_ge(S.pob, 1)
+            v.tensor_copy(off[1][:], T.pb[:, 0:2 * PC * N]).then_inc(S.pab, 1)
+        v.wait_ge(s2("pa", b), 1)
+        v.wait_ge(s2("y", 0, b), 1)
+        product(0, b, 0 if b else MINE, PC)
+    v.wait_ge(S.lds1, 32)
+    v.wait_ge(S.pab, 1)
+    for n in range(1, len(phases)):
+        x, t = phases[n]
+        steps = end_steps(*phases[n - 1])
+        if t:
+            v.wait_ge(s2("kb", x), t)
+        for p, (a, z) in enumerate(zip(CUTS, CUTS[1:])):
+            b = a // PC
+            if p == 0:
+                v.wait_ge(s2("yf", x), t + x)
+            elif p == 1 or a % PC == 0:
+                v.wait_ge(s2("y", x, b), t + 1)
+            product(x, b, a - PC * b, z - PC * b)
+            if 1 <= p <= len(steps):
+                steps[p - 1]()
+    steps = end_steps(1, R - 1)
+    results(0)
+    for step in steps:
+        step()
+    results(1)
+
+    for x in range(2):
+        sp.wait_ge(s2("kb", x), R)
+        sp.dma_start(T.left[half[x], :], sw[x][half[x], :]).then_inc(S.stl, 16)
+    act.wait_ge(S.fin, 4)
     act.dma_start(T.win[:], T.winf[0:128:16, 0:R]).then_inc(S.sts, 16)
     act.dma_start(T.score[:], T.scf[0:128:16, 0:R]).then_inc(S.sts, 16)
-    sp.wait_ge(S.stl, 16)
+    sp.wait_ge(S.stl, 32)
     act.wait_ge(S.sts, 32)
     g.wait_ge(S.lsent, nall)
     g.wait_ge(S.rsent, total)

@@ -2,13 +2,18 @@ from concourse.bass import DstId, RemoteDMATransfer
 from concourse.mybir import AluOpType, AxisListType, ActivationFunctionType
 
 N, KC, W, V, R = 4, 64, 4096, 2048, 3
-F = 288
+F = 256
 YO = 64
 H = 64
 PC = 32
 BL = 16 * PC
-CUTS = [0, 16, 32, 42, 52, 64, 74, 84, 96, 128]
-MINE = 8
+FIRST = [0, 8, 32, 44, 64, 80, 96, 112, 128]
+CUTS = [0, 20, 36, 46, 58, 70, 84, 108, 128]
+E = 7
+LATER = [0, 20, 36, 46, 56, 68, 80, 102, PC * N - E]
+BANK = 512
+ENDS = 36
+SHARE = 2560
 
 SCRATCH = {
     "wi": ("sbuf", [128, 16], "int32"),
@@ -18,12 +23,12 @@ SCRATCH = {
     "pn": ("sbuf", [128, 1], "int32"),
     "pi": ("sbuf", [128, 4], "int32"),
     "pc": ("sbuf", [128, 4], "bfloat16"),
-    "sp": ("sbuf", [128, 1], "float32"),
-    "ones": ("sbuf", [128, 128], "bfloat16"),
-    "idx": ("sbuf", [128, 256], "bfloat16"),
+    "top": ("sbuf", [128, 128], "bfloat16"),
+    "late": ("sbuf", [128, 128], "bfloat16"),
+    "step": ("sbuf", [128, KC], "bfloat16"),
+    "idx": ("sbuf", [128, 272], "bfloat16"),
     "zer": ("sbuf", [128, 16], "bfloat16"),
     "nk": ("sbuf", [128, 8], "float32"),
-    "hi": ("sbuf", [128, 8], "int32"),
     "co": ("sbuf", [128, 16], "uint16"),
     "winf": ("sbuf", [128, 4], "float32"),
     "scf": ("sbuf", [128, 4], "float32"),
@@ -31,26 +36,26 @@ SCRATCH = {
     "pa1": ("psum", [128, 512], "float32"),
     "pb": ("psum", [128, 512], "float32"),
 }
-for _n in ("los", "th", "im", "tb", "tn", "e0", "e1", "mb0", "mb1", "my0", "my1", "blk", "nb", "ny", "wf"):
+for _n in ("los", "th", "im", "tb", "tn", "e0", "e1", "mb0", "mb1", "my0", "my1", "blk", "nb", "ny", "wf", "wt", "wl2"):
     SCRATCH[_n] = ("sbuf", [128, 128], "bfloat16")
 for _x in range(2):
     SCRATCH["sw%d" % _x] = ("sbuf", [128, W], "bfloat16")
     SCRATCH["yg%d" % _x] = ("sbuf", [128, N * BL], "bfloat16")
     SCRATCH["pr%d" % _x] = ("sbuf", [128, N * BL], "bfloat16")
-    SCRATCH["off%d" % _x] = ("sbuf", [128, 2 * PC * N], "uint16")
-    SCRATCH["tab%d" % _x] = ("sbuf", [128, F + 256], "float32")
+    SCRATCH["off%d" % _x] = ("sbuf", [128, 2, PC * N], "uint16")
+    SCRATCH["tab%d" % _x] = ("sbuf", [128, 2 * F], "float32")
     SCRATCH["wb%d" % _x] = ("sbuf", [128, 16], "uint16")
-    SCRATCH["key%d" % _x] = ("psum", [128, 512], "float32")
-    SCRATCH["tp%d" % _x] = ("psum", [128, 512], "float32")
+    SCRATCH["key%d" % _x] = ("psum", [128, 2 * BANK], "float32")
 for _q in range(N):
     SCRATCH["lst%d" % _q] = ("sbuf", [128, 16], "uint16")
     SCRATCH["rep%d" % _q] = ("sbuf", [128, KC], "bfloat16")
 
-SEMAPHORES = (["ldw", "ldp", "conv", "vone", "vzer", "g1", "g2", "g3", "g4", "gix", "c1", "c2", "c3", "m1", "m2", "m3",
-               "m4", "m5", "m6", "swf", "go", "go2", "lsent", "rsent", "yd", "fin", "stl", "sts", "pob", "pab"]
-              + [n + str(x) for x in range(2) for n in ("lds", "tm", "tabs", "pk", "red", "hs", "cs", "ws", "ka", "kb", "yf")]
+SEMAPHORES = (["ldw", "ldp", "conv", "vone", "vzer", "g1", "g2", "g3", "g4", "gix", "c1", "c2", "m1", "m2", "m3",
+               "m4", "m5", "m6", "swf", "go2", "lsent", "rsent", "fin", "stl", "sts", "pob2", "pob3", "pab", "dup", "go", "dum"]
+              + [n + str(x) for x in range(2) for n in ("lds", "tm", "tabs", "pk", "red", "cs", "ws", "ka", "kb", "mv")]
               + [n + str(q) for q in range(N) for n in ("lst", "rp", "pg", "po", "pa")]
-              + [n + str(x) + str(b) for x in range(2) for b in range(N) for n in ("y", "pb")])
+              + [n + str(p) for p in range(len(FIRST) - 1) for n in ("yf", "pf")]
+              + [n + str(x) + str(p) for x in range(2) for p in range(len(CUTS) - 1) for n in ("y", "pb")])
 
 
 def rank_program(g, core, T, topo):
@@ -73,10 +78,10 @@ def rank_program(g, core, T, topo):
     mask = topo.mask(core, cores[others[0]])
     for q in others:
         mask &= topo.mask(core, cores[q])
-    nall = len([e for e in topo.engines(core, cores[others[0]]) if mask >> e & 1])
+    nall = len([e for e in topo.engines(core, cores[others[0]]) if mask >> e & 1]) * 2
 
     sw, yg, pr, off = [T.sw0, T.sw1], [T.yg0, T.yg1], [T.pr0, T.pr1], [T.off0, T.off1]
-    tab, wb, key, tp = [T.tab0, T.tab1], [T.wb0, T.wb1], [T.key0, T.key1], [T.tp0, T.tp1]
+    tab, wb, key, tp = [T.tab0, T.tab1], [T.wb0, T.wb1], [T.key0, T.key1], [T.key0, T.key1]
     pa = [T.pa0, T.pa1]
     half = [slice(0, H), slice(H, 2 * H)]
     phases = [(x, t) for t in range(R) for x in range(2)]
@@ -84,118 +89,162 @@ def rank_program(g, core, T, topo):
     def s2(name, *k):
         return S[name + "".join(str(i) for i in k)]
 
+    def pieces(n):
+        x, t = phases[n]
+        if n == 0:
+            return [(a, z, s2("yf", p), s2("pf", p), 1) for p, (a, z) in enumerate(zip(FIRST, FIRST[1:]))]
+        cuts = LATER if t else CUTS
+        return [(a, z, s2("y", x, p), s2("pb", x, p), t + x) for p, (a, z) in enumerate(zip(cuts, cuts[1:]))]
+
     sp.dma_start(T.wi[:], T.want[:]).then_inc(S.ldw, 16)
-    sp.dma_start(T.pepw[:], T.pep[:]).then_inc(S.ldp, 16)
-    for x, gate in ((0, S.go), (1, S.go2)):
-        sp.wait_ge(gate, 1)
-        for h in range(2):
-            sp.dma_start(sw[x][half[h], :], T.spec[half[x], :]).then_inc(s2("lds", x), 16)
+    sp.dma_start(sw[0][half[0], :], T.spec[half[0], :]).then_inc(S.lds0, 16)
+    sp.dma_start(T.pepw[:, 0:V // 2], T.pep[:, 0:V // 2]).then_inc(S.ldp, 16)
+    sp.wait_ge(S.go, 1)
+    sp.dma_start(T.pepw[:, V // 2:V], T.pep[:, V // 2:V]).then_inc(S.ldp, 16)
+    sp.wait_ge(S.rsent, nall)
+    for h in range(2):
+        sp.dma_start(sw[1][half[h], :], T.spec[half[1], :]).then_inc(S.lds1, 16)
+    for x in range(2):
+        sp.wait_ge(s2("pk", x), N)
+        for w in range(2):
+            for h in range(2):
+                sp.dma_start(off[x][H + 7 + 8 * h:2 * H:16, w, 0:16 * E],
+                             off[x][half[h], w, PC * N - E:PC * N]).then_inc(s2("mv", x), 16)
+
+    def iota(out, pattern, sem):
+        g.iota(out, pattern, 0, 0, allow_small_or_imprecise_dtypes=True).then_inc(sem, 1)
 
     g.iota(T.pn[:], [[0, 1]], 0, 1).then_inc(S.g1, 1)
-    g.iota(T.los[:], [[0, 2], [1, 8], [0, 8]], 0, 0, allow_small_or_imprecise_dtypes=True).then_inc(S.g2, 1)
-    g.iota(T.th[:], [[8, 2], [0, 8], [1, 8]], 0, 0, allow_small_or_imprecise_dtypes=True).then_inc(S.g3, 1)
+    iota(T.los[:], [[0, 2], [1, 8], [0, 8]], S.g2)
+    iota(T.th[:], [[8, 2], [0, 8], [1, 8]], S.g3)
     g.wait_ge(S.conv, 1)
     ids = []
-    for q in sends:
+    for q in order[1:]:
         rid, pid, _ = topo.addr(cores[q])
         ids.append(DstId(rid=rid, pnc=pid))
     land = T["lst%d" % rank]
-    g.remote_dma_fused([RemoteDMATransfer(dst_ids=ids, dma_engine_mask=mask, remote_sem=s2("lst", rank),
-                                          srcs=[T.wl[:]], dsts=[land[:] for q in sends])], local_sem=S.lsent)
+    for part in (ids[:1], ids[1:]):
+        g.remote_dma_fused([RemoteDMATransfer(dst_ids=part, dma_engine_mask=mask, remote_sem=s2("lst", rank),
+                                              srcs=[T.wl[:]], dsts=[land[:] for q in part])], local_sem=S.lsent)
     g.sem_inc(S.go, 1)
-    g.iota(T.im[:], [[0, 8], [1, 16]], 0, 0, allow_small_or_imprecise_dtypes=True).then_inc(S.g4, 1)
+    iota(T.im[:], [[0, 8], [1, 16]], S.g4)
     total = 0
-    for q in sends:
-        g.wait_ge(s2("pg", q), 1)
-        rid, pid, _ = topo.addr(cores[q])
-        g.remote_dma(T.mas[:, KC * rank:KC * rank + KC], T["rep%d" % q][:], s2("rp", rank), S.rsent, pid, rid,
-                     topo.mask(core, cores[q]))
-        total += len(topo.engines(core, cores[q]))
-    g.sem_inc(S.go2, 1)
-    g.iota(T.idx[0:1, 0:256], [[-1, 256]], 0, 0, allow_small_or_imprecise_dtypes=True).then_inc(S.gix, 1)
+    for call in (sends[:1], sends[1:]):
+        moves = []
+        for k, q in enumerate(call):
+            g.wait_ge(s2("pg", q), 1)
+            rid, pid, _ = topo.addr(cores[q])
+            eng = topo.engines(core, cores[q])
+            eng = eng[k * len(eng) // len(call):(k + 1) * len(eng) // len(call)]
+            moves.append(RemoteDMATransfer(dst_ids=[DstId(rid=rid, pnc=pid)], dma_engine_mask=sum(1 << e for e in eng),
+                                           remote_sem=s2("rp", rank), src=T["rep%d" % q][:],
+                                           dst=T.mas[:, KC * rank:KC * rank + KC]))
+            total += len(eng)
+        g.remote_dma_fused(moves, local_sem=S.rsent)
+    iota(T.idx[0:1, 0:256], [[-1, 256]], S.gix)
+    g.iota(T.idx[0:1, 256:256 + 2 * E], [[-1, 2], [-2, E]], -(KC * order[-1] + KC - 2 * E), 0,
+           allow_small_or_imprecise_dtypes=True).then_inc(S.gix, 1)
+    iota(T.late[0:1, 0:H], [[0, 4], [1, 2], [0, 8]], S.gix)
 
-    def bins_mm(x, b, bank):
-        q, c = order[b], 2 * PC * b
+    def bins_mm(x, b, bank, col, gap):
+        q = order[b]
         for w, mats in enumerate(((T.mb0, T.mb1), (T.my0, T.my1))):
             for s in range(2):
-                mm = pe.matmul(bank[:, c + PC * w:c + PC * w + PC], mats[s][half[x], :],
+                mm = pe.matmul(bank[:, col + gap * w:col + gap * w + PC], mats[s][half[x], :],
                                T.mas[half[x], KC * q + s:KC * q + KC:2], s == 0, s == 1)
         return mm
 
     def tab_mm(x):
-        pe.matmul(tp[x][:, 0:256], T.nb[half[x], :], T.mas[half[x], :], True, True)
-        pe.matmul(tp[x][:, 256:512], T.ny[half[x], :], T.mas[half[x], :], True, True).then_inc(s2("tm", x), 1)
+        pe.matmul(tp[x][:, BANK:BANK + F], T.nb[half[x], :], T.mas[half[x], :], True, True)
+        pe.matmul(tp[x][:, BANK + F:2 * BANK], T.ny[half[x], :], T.mas[half[x], :], True, True).then_inc(s2("tm", x), 1)
 
     pe.wait_ge(S.m3, 2)
     for b, q in enumerate(order):
-        pe.wait_ge(s2("rp" if b else "pg", q), nin[q] if b else 1)
+        pe.wait_ge(s2("rp" if b else "pg", q), nin[q] // (1 + far(q)) if b else 1)
         if b >= 2:
             pe.wait_ge(s2("pa", b - 2), 1)
-        bins_mm(0, b, pa[b % 2]).then_inc(s2("po", b), 1)
-        mm = bins_mm(1, b, T.pb)
-    mm.then_inc(S.pob, 1)
-    pe.wait_ge(S.swf, 1)
-    pe.wait_ge(S.gix, 1)
-    pe.wait_ge(S.vone, 1)
+        bins_mm(0, b, pa[b % 2], 0, PC).then_inc(s2("po", b), 1)
+        if b < 3:
+            mm = bins_mm(1, b, T.pb, PC * b, PC * 3)
+        else:
+            mm = bins_mm(1, b, T.key1, 0, PC)
+        if b >= 2:
+            mm.then_inc(s2("pob", b), 1)
     pe.wait_ge(S.m6, 1)
-    done = {}
+    tab_mm(0)
+    pe.wait_ge(S.swf, 5)
+    pe.wait_ge(S.gix, 3)
+    pe.wait_ge(S.vone, 4)
     for n, (x, t) in enumerate(phases):
+        if n == 1:
+            pe.wait_ge(S.pab, 2)
         if t:
             pe.wait_ge(s2("red", x), t)
+        moved = [(s, i, r) for s in range(2) for i in range(8) for r in (7, 15)] if t else []
+        if t:
+            pe.wait_ge(s2("tabs", x), 2)
+            pe.matmul(key[x][:, BANK:BANK + 2 * E], T.top[0:1, :], T.idx[0:1, 256:256 + 2 * E], True, False)
+            pe.matmul(key[x][:, BANK:BANK + 2 * E], T.late[0:1, :], T.step[0:1, 0:2 * E], False, False)
         for b, q in enumerate(order):
-            dst = key[x][:, KC * q:KC * q + KC]
-            pe.matmul(dst, T.ones[0:1, 0:128], T.idx[0:1, KC * q:KC * q + KC], True, False)
-            cuts = [c for c in CUTS[:-1] if c // PC == b]
-            done[x, b] = done.get((x, b), 0) + (len(cuts) if n else 1 if b else 2)
-            pe.wait_ge(s2("pb", x, b), done[x, b])
+            wide = KC - 2 * E if t and b == N - 1 else KC
+            first = BANK - 256 + (2 * E if t else 0) + KC * b
+            dst = key[x][:, first:first + wide]
+            pe.matmul(dst, T.top[0:1, :], T.idx[0:1, KC * q:KC * q + wide], True, False)
+            pe.matmul(dst, T.late[0:1, :], T.step[0:1, 0:wide], False, False)
+            for a, z, _, made, count in pieces(n):
+                if a < PC * (b + 1) and z > PC * b:
+                    pe.wait_ge(made, count)
+                    have = z
             for i in range(8):
-                mm = pe.matmul(dst, T.wf[:], pr[x][:, BL * b + i:BL * (b + 1):8], False, i == 7)
+                mm = pe.matmul(dst, T.wt[:] if t and i == 7 else T.wf[:], pr[x][:, BL * b + i:BL * b + 8 * wide:8],
+                               False, i == 7)
+            while moved and E * (8 * moved[0][0] + moved[0][1] + 1) <= have:
+                s, i, r = moved.pop(0)
+                c = 16 * E * (8 * s + i) + r
+                mm = pe.matmul(key[x][:, BANK + E * s:BANK + E * s + E], T.wl2[:], pr[x][:, c:c + 16 * E - 15:16],
+                               False, not moved)
             mm.then_inc(s2("pk", x), 1)
-            if n == 0 and b == 1:
-                tab_mm(0)
-            if n == 1 and b == 0:
-                tab_mm(1)
+        if n == 0:
+            tab_mm(1)
 
-    def ygather(x, b, a, z, sem):
-        c = 2 * PC * b + PC
-        act.activation(yg[x][:, BL * b + 16 * a:BL * b + 16 * z],
-                       sw[x][:, YO:W].indirect(off[x][:, c + a:c + z]), copy).then_inc(sem, 1)
+    def table(x, w):
+        act.wait_ge(s2("tm", x), 1)
+        act.activation(tab[x][:, F * w:F * w + F], tp[x][:, BANK + F * w:BANK + F * w + F], copy).then_inc(s2("tabs", x), 1)
 
+    act.wait_ge(S.lds0, 16)
+    act.activation(sw[0][half[1], SHARE:W], sw[0][half[0], SHARE:W], copy).then_inc(S.dup, 1)
     act.wait_ge(S.m4, 1)
     act.activation(T.wf[:], T.blk[:], copy, scale=float(F)).then_inc(S.swf, 1)
+    for h in range(2):
+        act.activation(T.wt[half[h], :], T.blk[half[h], :], copy, scale=float(F * (1 - h))).then_inc(S.swf, 1)
+        act.activation(T.wl2[half[h], :], T.blk[half[h], :], copy, scale=float(F * h)).then_inc(S.swf, 1)
+    act.wait_ge(S.dup, 2)
     for n, (x, t) in enumerate(phases):
-        if t == 0:
-            act.wait_ge(s2("lds", x), 32)
-        else:
-            act.wait_ge(s2("kb", x), t)
         if n == 1:
-            act.wait_ge(S.pab, 1)
-        for b in range(N):
-            if n == 0:
-                act.wait_ge(s2("pa", b), 1)
-                ygather(x, b, 0 if b else MINE, PC, s2("y", x, b))
-            elif b == 0:
-                ygather(x, b, 0, PC // 2, s2("yf", x))
-                ygather(x, b, PC // 2, PC, s2("y", x, b))
-            else:
-                ygather(x, b, 0, PC, s2("y", x, b))
-            if n in (1, 2) and b == 1:
-                o = 1 - x
-                act.wait_ge(s2("tm", o), 1)
-                act.activation(tab[o][:, 0:256], tp[o][:, 0:256], copy).then_inc(s2("tabs", o), 1)
-                act.activation(tab[o][:, F:F + 256], tp[o][:, 256:512], copy).then_inc(s2("tabs", o), 1)
+            act.wait_ge(S.pab, 2)
+            act.wait_ge(S.lds1, 32)
+        if t == 1:
+            act.wait_ge(s2("mv", x), 64)
+        if t:
+            act.wait_ge(s2("kb", x), t)
+        for a, z, got, _, _ in pieces(n):
+            if n == 0 and a % PC == 0:
+                act.wait_ge(s2("pa", a // PC), 1)
+            act.activation(yg[x][:, 16 * a:16 * z], sw[x][:, YO:W].indirect(off[x][:, 1, a:z]), copy).then_inc(got, 1)
+            if n in (1, 2) and z in CUTS[2:4]:
+                table(1 - x, CUTS.index(z) - 2)
 
     v.wait_ge(S.g1, 1)
     v.tensor_scalar(T.pi[:, 0:1], T.pn[:], 15, None, op.bitwise_and).then_inc(S.c1, 1)
     v.tensor_scalar(T.pi[:, 1:2], T.pn[:], 3, 6, op.logical_shift_right, op.bitwise_and).then_inc(S.c1, 1)
-    v.tensor_scalar(T.pi[:, 2:3], T.pn[:], 8, None, op.bitwise_and).then_inc(S.c1, 1)
-    v.memset(T.ones[0:1, :], 1.0).then_inc(S.vone, 1)
-    v.memset(T.zer[:], 0.0).then_inc(S.vzer, 1)
-    v.wait_ge(S.c1, 3)
+    v.memset(T.top[0:1, 0:H], 1.0).then_inc(S.vone, 1)
+    v.memset(T.top[0:1, H:2 * H], 0.0).then_inc(S.vone, 1)
+    v.memset(T.late[0:1, H:2 * H], 0.0).then_inc(S.vone, 1)
+    v.wait_ge(S.c1, 2)
     v.tensor_copy(T.pc[:, 0:2], T.pi[:, 0:2]).then_inc(S.c2, 1)
-    v.tensor_scalar(T.sp[:], T.pi[:, 2:3], -F / 8.0, -128.0, op.mult, op.add).then_inc(S.c3, 1)
-    for x in range(2):
-        v.memset(tab[x][:, 256:F], 0.0).then_inc(S.vzer, 1)
+    v.memset(T.step[0:1, :], -float(F)).then_inc(S.vone, 1)
+    v.memset(T.zer[:], 0.0).then_inc(S.vzer, 1)
+    v.memset(T.co[:], 0).then_inc(S.vzer, 1)
     v.wait_ge(S.c2, 1)
     row, two = T.pc[:, 0:1], T.pc[:, 1:2]
     v.wait_ge(S.g2, 1)
@@ -212,54 +261,48 @@ def rank_program(g, core, T, topo):
     v.wait_ge(S.m2, 2)
     v.tensor_tensor(T.my0[:], T.e0[:], T.mb0[:], op.subtract).then_inc(S.m3, 1)
     v.tensor_tensor(T.my1[:], T.e1[:], T.mb1[:], op.subtract).then_inc(S.m3, 1)
-    v.wait_ge(S.conv, 1)
-    v.wait_ge(S.ldp, 16)
-    v.tensor_copy(T.mas[:, KC * rank:KC * rank + KC],
-                  T.pepw[:].indirect(T.wl[:, 4 * rank:4 * rank + 4])).then_inc(s2("pg", rank), 1)
+    v.wait_ge(S.lds0, 16)
+    v.tensor_copy(sw[0][half[1], 0:SHARE], sw[0][half[0], 0:SHARE]).then_inc(S.dup, 1)
     v.wait_ge(S.g4, 1)
     v.tensor_scalar(T.tn[:], T.im[:], row, None, op.is_ge).then_inc(S.m5, 1)
-    v.wait_ge(S.m4, 1)
-    v.wait_ge(S.m5, 1)
-    v.tensor_tensor(T.nb[:], T.tn[:], T.blk[:], op.mult).then_inc(S.m5, 1)
-
-    def pack(b):
-        c = 2 * PC * b
-        v.wait_ge(s2("po", b), 1)
-        v.tensor_copy(off[0][:, c:c + 2 * PC], pa[b % 2][:, c:c + 2 * PC]).then_inc(s2("pa", b), 1)
-
-    pack(0)
+    v.wait_ge(S.conv, 1)
+    v.wait_ge(S.ldp, 32)
+    v.tensor_copy(T.mas[:, KC * rank:KC * rank + KC],
+                  T.pepw[:].indirect(T.wl[:, 4 * rank:4 * rank + 4])).then_inc(s2("pg", rank), 1)
     for q in sends:
         v.wait_ge(s2("lst", q), nin[q])
         v.tensor_copy(T["rep%d" % q][:],
                       T.pepw[:].indirect(T["lst%d" % q][:, 4 * rank:4 * rank + 4])).then_inc(s2("pg", q), 1)
+
+    def pack(b):
+        v.wait_ge(s2("po", b), 1)
+        v.tensor_copy(off[0][:, :, PC * b:PC * b + PC], pa[b % 2][:, 0:2 * PC]).then_inc(s2("pa", b), 1)
+
+    pack(0)
+    v.wait_ge(S.m4, 1)
+    v.wait_ge(S.m5, 1)
+    v.tensor_tensor(T.nb[:], T.tn[:], T.blk[:], op.mult).then_inc(S.m5, 1)
     v.wait_ge(S.m5, 2)
     v.tensor_tensor(T.ny[:], T.blk[:], T.nb[:], op.subtract).then_inc(S.m6, 1)
-    v.wait_ge(S.vzer, 3)
-    v.wait_ge(S.c3, 1)
-
-    def product(x, b, a, z):
-        c = 2 * PC * b
-        v.tensor_tensor(pr[x][:, BL * b + 16 * a:BL * b + 16 * z], sw[x][:].indirect(off[x][:, c + a:c + z]),
-                        yg[x][:, BL * b + 16 * a:BL * b + 16 * z], op.mult).then_inc(s2("pb", x, b), 1)
+    v.wait_ge(S.vzer, 2)
 
     def end_steps(x, t):
         k = R * x + t
-        nk, hi, co = T.nk[:, k:k + 1], T.hi[:, k:k + 1], T.co[:, 2 * k:2 * k + 1]
+        nk, co = T.nk[:, k:k + 1], T.co[:, 2 * k:2 * k + 1]
 
         def best():
             v.wait_ge(s2("pk", x), N * (t + 1))
-            v.tensor_reduce(nk, key[x][:, 0:256], AxisListType.X, op.max, negate=True).then_inc(s2("red", x), 1)
-
-        def score():
-            v.wait_ge(s2("red", x), t + 1)
-            v.tensor_scalar(hi, nk, T.sp[:], 1.0 / F, op.add, op.mult).then_inc(s2("hs", x), 1)
+            first = BANK - 256 + (2 * E if t else 0)
+            v.tensor_reduce(nk, key[x][:, first:first + 256], AxisListType.X, op.max, negate=True).then_inc(s2("red", x), 1)
 
         def place():
-            v.wait_ge(s2("hs", x), t + 1)
-            v.tensor_scalar(co, hi, -float(F), nk, op.mult, op.add).then_inc(s2("cs", x), 1)
+            v.wait_ge(s2("red", x), t + 1)
+            for h in range(2) if t < R - 1 else [x]:
+                v.tensor_scalar(T.co[half[h], 2 * k:2 * k + 1], T.nk[half[0], k:k + 1], T.nk[half[1], k:k + 1], None,
+                                op.subtract).then_inc(s2("cs", x), 1)
 
         def fetch():
-            v.wait_ge(s2("cs", x), t + 1)
+            v.wait_ge(s2("cs", x), min(2 * t + 2, 2 * R - 1))
             if t == 0:
                 v.wait_ge(s2("tabs", x), 2)
             v.tensor_copy(wb[x][:], tab[x][:].indirect(co)).then_inc(s2("ws", x), 1)
@@ -272,46 +315,41 @@ def rank_program(g, core, T, topo):
             v.wait_ge(s2("ka", x), t + 1)
             v.tensor_copy(sw[x][:, YO:W].indirect(wb[x][:, 8:9]), T.zer[:]).then_inc(s2("kb", x), 1)
 
-        return [best, score, place, fetch, erase_b, erase_y]
+        return [best, place, fetch, erase_b, erase_y]
 
     def results(x):
         v.tensor_copy(T.winf[half[x], 0:R], T.co[half[x], 2 * R * x:2 * R * x + 2 * R:2]).then_inc(S.fin, 1)
-        v.tensor_scalar(T.scf[half[x], 0:R], T.hi[half[x], R * x:R * x + R], -1.0, None, op.mult).then_inc(S.fin, 1)
+        v.tensor_scalar(T.scf[half[x], 0:R], T.nk[half[1], R * x:R * x + R], -1.0 / F, None, op.mult).then_inc(S.fin, 1)
 
-    v.wait_ge(S.lds0, 32)
-    v.wait_ge(s2("pa", 0), 1)
-    v.tensor_copy(yg[0][:, 0:16 * MINE], sw[0][:, YO:W].indirect(off[0][:, PC:PC + MINE])).then_inc(S.yd, 1)
-    pack(1)
-    v.wait_ge(S.yd, 1)
-    product(0, 0, 0, MINE)
-    for b in range(N):
-        if 2 <= b + 1 < N:
-            pack(b + 1)
-        if b == 2:
-            v.wait_ge(S.pob, 1)
-            v.tensor_copy(off[1][:], T.pb[:, 0:2 * PC * N]).then_inc(S.pab, 1)
-        v.wait_ge(s2("pa", b), 1)
-        v.wait_ge(s2("y", 0, b), 1)
-        product(0, b, 0 if b else MINE, PC)
-    v.wait_ge(S.lds1, 32)
-    v.wait_ge(S.pab, 1)
-    for n in range(1, len(phases)):
-        x, t = phases[n]
-        steps = end_steps(*phases[n - 1])
+    v.wait_ge(S.dup, 2)
+    for n, (x, t) in enumerate(phases):
+        steps = end_steps(*phases[n - 1]) if n else []
+        if n == 1:
+            v.wait_ge(S.pab, 2)
+            v.wait_ge(S.lds1, 32)
+        if t == 1:
+            v.wait_ge(s2("mv", x), 64)
         if t:
             v.wait_ge(s2("kb", x), t)
-        for p, (a, z) in enumerate(zip(CUTS, CUTS[1:])):
-            b = a // PC
-            if p == 0:
-                v.wait_ge(s2("yf", x), t + x)
-            elif p == 1 or a % PC == 0:
-                v.wait_ge(s2("y", x, b), t + 1)
-            product(x, b, a - PC * b, z - PC * b)
-            if 1 <= p <= len(steps):
-                steps[p - 1]()
-    steps = end_steps(1, R - 1)
+        for a, z, got, made, count in pieces(n):
+            if n == 0 and a % PC == 0:
+                v.wait_ge(s2("pa", a // PC), 1)
+            v.wait_ge(got, count)
+            v.tensor_tensor(pr[x][:, 16 * a:16 * z], sw[x][:].indirect(off[x][:, 0, a:z]), yg[x][:, 16 * a:16 * z],
+                            op.mult).then_inc(made, 1)
+            if n == 0 and z in FIRST[1:5:2]:
+                pack(z // PC + 1)
+            if n == 0 and z == FIRST[4]:
+                v.wait_ge(S.pob2, 1)
+                v.tensor_copy(off[1][:, :, 0:3 * PC], T.pb[:, 0:6 * PC]).then_inc(S.pab, 1)
+                pack(3)
+            if n == 0 and z == FIRST[5]:
+                v.wait_ge(S.pob3, 1)
+                v.tensor_copy(off[1][:, :, 3 * PC:4 * PC], T.key1[:, 0:2 * PC]).then_inc(S.pab, 1)
+            if z >= ENDS and steps:
+                steps.pop(0)()
     results(0)
-    for step in steps:
+    for step in end_steps(1, R - 1):
         step()
     results(1)
 

from concourse.bass import DstId, RemoteDMATransfer
from concourse.mybir import AluOpType, AxisListType, ActivationFunctionType

N, KC, W, V, R = 4, 64, 4096, 2048, 3
F = 256
YO = 64
H = 64
PC = 32
BL = 16 * PC
FIRST = [0, 8, 32, 44, 64, 80, 96, 112, 128]
CUTS = [0, 20, 36, 46, 58, 70, 84, 108, 128]
E = 7
LATER = [0, 20, 36, 46, 56, 68, 80, 102, PC * N - E]
BANK = 512
ENDS = 36
SHARE = 2560

SCRATCH = {
    "wi": ("sbuf", [128, 16], "int32"),
    "wl": ("sbuf", [128, 16], "uint16"),
    "pepw": ("sbuf", [128, V], "bfloat16"),
    "mas": ("sbuf", [128, N * KC], "bfloat16"),
    "pn": ("sbuf", [128, 1], "int32"),
    "pi": ("sbuf", [128, 4], "int32"),
    "pc": ("sbuf", [128, 4], "bfloat16"),
    "top": ("sbuf", [128, 128], "bfloat16"),
    "late": ("sbuf", [128, 128], "bfloat16"),
    "step": ("sbuf", [128, KC], "bfloat16"),
    "idx": ("sbuf", [128, 272], "bfloat16"),
    "zer": ("sbuf", [128, 16], "bfloat16"),
    "nk": ("sbuf", [128, 8], "float32"),
    "co": ("sbuf", [128, 16], "uint16"),
    "winf": ("sbuf", [128, 4], "float32"),
    "scf": ("sbuf", [128, 4], "float32"),
    "pa0": ("psum", [128, 512], "float32"),
    "pa1": ("psum", [128, 512], "float32"),
    "pb": ("psum", [128, 512], "float32"),
}
for _n in ("los", "th", "im", "tb", "tn", "e0", "e1", "mb0", "mb1", "my0", "my1", "blk", "nb", "ny", "wf", "wt", "wl2"):
    SCRATCH[_n] = ("sbuf", [128, 128], "bfloat16")
for _x in range(2):
    SCRATCH["sw%d" % _x] = ("sbuf", [128, W], "bfloat16")
    SCRATCH["yg%d" % _x] = ("sbuf", [128, N * BL], "bfloat16")
    SCRATCH["pr%d" % _x] = ("sbuf", [128, N * BL], "bfloat16")
    SCRATCH["off%d" % _x] = ("sbuf", [128, 2, PC * N], "uint16")
    SCRATCH["tab%d" % _x] = ("sbuf", [128, 2 * F], "float32")
    SCRATCH["wb%d" % _x] = ("sbuf", [128, 16], "uint16")
    SCRATCH["key%d" % _x] = ("psum", [128, 2 * BANK], "float32")
for _q in range(N):
    SCRATCH["lst%d" % _q] = ("sbuf", [128, 16], "uint16")
    SCRATCH["rep%d" % _q] = ("sbuf", [128, KC], "bfloat16")

SEMAPHORES = (["ldw", "ldp", "conv", "vone", "vzer", "g1", "g2", "g3", "g4", "gix", "c1", "c2", "m1", "m2", "m3",
               "m4", "m5", "m6", "swf", "go2", "lsent", "rsent", "fin", "stl", "sts", "pob2", "pob3", "pab", "dup", "go", "dum"]
              + [n + str(x) for x in range(2) for n in ("lds", "tm", "tabs", "pk", "red", "cs", "ws", "ka", "kb", "mv")]
              + [n + str(q) for q in range(N) for n in ("lst", "rp", "pg", "po", "pa")]
              + [n + str(p) for p in range(len(FIRST) - 1) for n in ("yf", "pf")]
              + [n + str(x) + str(p) for x in range(2) for p in range(len(CUTS) - 1) for n in ("y", "pb")])


def rank_program(g, core, T, topo):
    rank = T.rank_of(core)
    if rank is None:
        return
    S = T.sem
    v, act, pe, sp = g.vector, g.scalar, g.tensor, g.sync
    op = AluOpType
    copy = ActivationFunctionType.Copy
    cores = T.cores

    def far(q):
        return 0 if topo.same_plane(topo.chip(cores[q]), topo.chip(core)) else 1

    others = [q for q in range(N) if q != rank]
    sends = sorted(others, key=lambda q: (far(q), (q - rank) % N))
    order = [rank] + sorted(others, key=lambda q: (far(q), (rank - q) % N))
    nin = {q: len(topo.engines(cores[q], core)) for q in others}
    mask = topo.mask(core, cores[others[0]])
    for q in others:
        mask &= topo.mask(core, cores[q])
    nall = len([e for e in topo.engines(core, cores[others[0]]) if mask >> e & 1]) * 2

    sw, yg, pr, off = [T.sw0, T.sw1], [T.yg0, T.yg1], [T.pr0, T.pr1], [T.off0, T.off1]
    tab, wb, key, tp = [T.tab0, T.tab1], [T.wb0, T.wb1], [T.key0, T.key1], [T.key0, T.key1]
    pa = [T.pa0, T.pa1]
    half = [slice(0, H), slice(H, 2 * H)]
    phases = [(x, t) for t in range(R) for x in range(2)]

    def s2(name, *k):
        return S[name + "".join(str(i) for i in k)]

    def pieces(n):
        x, t = phases[n]
        if n == 0:
            return [(a, z, s2("yf", p), s2("pf", p), 1) for p, (a, z) in enumerate(zip(FIRST, FIRST[1:]))]
        cuts = LATER if t else CUTS
        return [(a, z, s2("y", x, p), s2("pb", x, p), t + x) for p, (a, z) in enumerate(zip(cuts, cuts[1:]))]

    sp.dma_start(T.wi[:], T.want[:]).then_inc(S.ldw, 16)
    sp.dma_start(sw[0][half[0], :], T.spec[half[0], :]).then_inc(S.lds0, 16)
    sp.dma_start(T.pepw[:, 0:V // 2], T.pep[:, 0:V // 2]).then_inc(S.ldp, 16)
    sp.wait_ge(S.go, 1)
    sp.dma_start(T.pepw[:, V // 2:V], T.pep[:, V // 2:V]).then_inc(S.ldp, 16)
    sp.wait_ge(S.rsent, nall)
    for h in range(2):
        sp.dma_start(sw[1][half[h], :], T.spec[half[1], :]).then_inc(S.lds1, 16)
    for x in range(2):
        sp.wait_ge(s2("pk", x), N)
        for w in range(2):
            for h in range(2):
                sp.dma_start(off[x][H + 7 + 8 * h:2 * H:16, w, 0:16 * E],
                             off[x][half[h], w, PC * N - E:PC * N]).then_inc(s2("mv", x), 16)

    def iota(out, pattern, sem):
        g.iota(out, pattern, 0, 0, allow_small_or_imprecise_dtypes=True).then_inc(sem, 1)

    g.iota(T.pn[:], [[0, 1]], 0, 1).then_inc(S.g1, 1)
    iota(T.los[:], [[0, 2], [1, 8], [0, 8]], S.g2)
    iota(T.th[:], [[8, 2], [0, 8], [1, 8]], S.g3)
    g.wait_ge(S.conv, 1)
    ids = []
    for q in order[1:]:
        rid, pid, _ = topo.addr(cores[q])
        ids.append(DstId(rid=rid, pnc=pid))
    land = T["lst%d" % rank]
    for part in (ids[:1], ids[1:]):
        g.remote_dma_fused([RemoteDMATransfer(dst_ids=part, dma_engine_mask=mask, remote_sem=s2("lst", rank),
                                              srcs=[T.wl[:]], dsts=[land[:] for q in part])], local_sem=S.lsent)
    g.sem_inc(S.go, 1)
    iota(T.im[:], [[0, 8], [1, 16]], S.g4)
    total = 0
    for call in (sends[:1], sends[1:]):
        moves = []
        for k, q in enumerate(call):
            g.wait_ge(s2("pg", q), 1)
            rid, pid, _ = topo.addr(cores[q])
            eng = topo.engines(core, cores[q])
            eng = eng[k * len(eng) // len(call):(k + 1) * len(eng) // len(call)]
            moves.append(RemoteDMATransfer(dst_ids=[DstId(rid=rid, pnc=pid)], dma_engine_mask=sum(1 << e for e in eng),
                                           remote_sem=s2("rp", rank), src=T["rep%d" % q][:],
                                           dst=T.mas[:, KC * rank:KC * rank + KC]))
            total += len(eng)
        g.remote_dma_fused(moves, local_sem=S.rsent)
    iota(T.idx[0:1, 0:256], [[-1, 256]], S.gix)
    g.iota(T.idx[0:1, 256:256 + 2 * E], [[-1, 2], [-2, E]], -(KC * order[-1] + KC - 2 * E), 0,
           allow_small_or_imprecise_dtypes=True).then_inc(S.gix, 1)
    iota(T.late[0:1, 0:H], [[0, 4], [1, 2], [0, 8]], S.gix)

    def bins_mm(x, b, bank, col, gap):
        q = order[b]
        for w, mats in enumerate(((T.mb0, T.mb1), (T.my0, T.my1))):
            for s in range(2):
                mm = pe.matmul(bank[:, col + gap * w:col + gap * w + PC], mats[s][half[x], :],
                               T.mas[half[x], KC * q + s:KC * q + KC:2], s == 0, s == 1)
        return mm

    def tab_mm(x):
        pe.matmul(tp[x][:, BANK:BANK + F], T.nb[half[x], :], T.mas[half[x], :], True, True)
        pe.matmul(tp[x][:, BANK + F:2 * BANK], T.ny[half[x], :], T.mas[half[x], :], True, True).then_inc(s2("tm", x), 1)

    pe.wait_ge(S.m3, 2)
    for b, q in enumerate(order):
        pe.wait_ge(s2("rp" if b else "pg", q), nin[q] // (1 + far(q)) if b else 1)
        if b >= 2:
            pe.wait_ge(s2("pa", b - 2), 1)
        bins_mm(0, b, pa[b % 2], 0, PC).then_inc(s2("po", b), 1)
        if b < 3:
            mm = bins_mm(1, b, T.pb, PC * b, PC * 3)
        else:
            mm = bins_mm(1, b, T.key1, 0, PC)
        if b >= 2:
            mm.then_inc(s2("pob", b), 1)
    pe.wait_ge(S.m6, 1)
    tab_mm(0)
    pe.wait_ge(S.swf, 5)
    pe.wait_ge(S.gix, 3)
    pe.wait_ge(S.vone, 4)
    for n, (x, t) in enumerate(phases):
        if n == 1:
            pe.wait_ge(S.pab, 2)
        if t:
            pe.wait_ge(s2("red", x), t)
        moved = [(s, i, r) for s in range(2) for i in range(8) for r in (7, 15)] if t else []
        if t:
            pe.wait_ge(s2("tabs", x), 2)
            pe.matmul(key[x][:, BANK:BANK + 2 * E], T.top[0:1, :], T.idx[0:1, 256:256 + 2 * E], True, False)
            pe.matmul(key[x][:, BANK:BANK + 2 * E], T.late[0:1, :], T.step[0:1, 0:2 * E], False, False)
        for b, q in enumerate(order):
            wide = KC - 2 * E if t and b == N - 1 else KC
            first = BANK - 256 + (2 * E if t else 0) + KC * b
            dst = key[x][:, first:first + wide]
            pe.matmul(dst, T.top[0:1, :], T.idx[0:1, KC * q:KC * q + wide], True, False)
            pe.matmul(dst, T.late[0:1, :], T.step[0:1, 0:wide], False, False)
            for a, z, _, made, count in pieces(n):
                if a < PC * (b + 1) and z > PC * b:
                    pe.wait_ge(made, count)
                    have = z
            for i in range(8):
                mm = pe.matmul(dst, T.wt[:] if t and i == 7 else T.wf[:], pr[x][:, BL * b + i:BL * b + 8 * wide:8],
                               False, i == 7)
            while moved and E * (8 * moved[0][0] + moved[0][1] + 1) <= have:
                s, i, r = moved.pop(0)
                c = 16 * E * (8 * s + i) + r
                mm = pe.matmul(key[x][:, BANK + E * s:BANK + E * s + E], T.wl2[:], pr[x][:, c:c + 16 * E - 15:16],
                               False, not moved)
            mm.then_inc(s2("pk", x), 1)
        if n == 0:
            tab_mm(1)

    def table(x, w):
        act.wait_ge(s2("tm", x), 1)
        act.activation(tab[x][:, F * w:F * w + F], tp[x][:, BANK + F * w:BANK + F * w + F], copy).then_inc(s2("tabs", x), 1)

    act.wait_ge(S.lds0, 16)
    act.activation(sw[0][half[1], SHARE:W], sw[0][half[0], SHARE:W], copy).then_inc(S.dup, 1)
    act.wait_ge(S.m4, 1)
    act.activation(T.wf[:], T.blk[:], copy, scale=float(F)).then_inc(S.swf, 1)
    for h in range(2):
        act.activation(T.wt[half[h], :], T.blk[half[h], :], copy, scale=float(F * (1 - h))).then_inc(S.swf, 1)
        act.activation(T.wl2[half[h], :], T.blk[half[h], :], copy, scale=float(F * h)).then_inc(S.swf, 1)
    act.wait_ge(S.dup, 2)
    for n, (x, t) in enumerate(phases):
        if n == 1:
            act.wait_ge(S.pab, 2)
            act.wait_ge(S.lds1, 32)
        if t == 1:
            act.wait_ge(s2("mv", x), 64)
        if t:
            act.wait_ge(s2("kb", x), t)
        for a, z, got, _, _ in pieces(n):
            if n == 0 and a % PC == 0:
                act.wait_ge(s2("pa", a // PC), 1)
            act.activation(yg[x][:, 16 * a:16 * z], sw[x][:, YO:W].indirect(off[x][:, 1, a:z]), copy).then_inc(got, 1)
            if n in (1, 2) and z in CUTS[2:4]:
                table(1 - x, CUTS.index(z) - 2)

    v.wait_ge(S.g1, 1)
    v.tensor_scalar(T.pi[:, 0:1], T.pn[:], 15, None, op.bitwise_and).then_inc(S.c1, 1)
    v.tensor_scalar(T.pi[:, 1:2], T.pn[:], 3, 6, op.logical_shift_right, op.bitwise_and).then_inc(S.c1, 1)
    v.memset(T.top[0:1, 0:H], 1.0).then_inc(S.vone, 1)
    v.memset(T.top[0:1, H:2 * H], 0.0).then_inc(S.vone, 1)
    v.memset(T.late[0:1, H:2 * H], 0.0).then_inc(S.vone, 1)
    v.wait_ge(S.c1, 2)
    v.tensor_copy(T.pc[:, 0:2], T.pi[:, 0:2]).then_inc(S.c2, 1)
    v.memset(T.step[0:1, :], -float(F)).then_inc(S.vone, 1)
    v.memset(T.zer[:], 0.0).then_inc(S.vzer, 1)
    v.memset(T.co[:], 0).then_inc(S.vzer, 1)
    v.wait_ge(S.c2, 1)
    row, two = T.pc[:, 0:1], T.pc[:, 1:2]
    v.wait_ge(S.g2, 1)
    v.tensor_scalar(T.e0[:], T.los[:], two, None, op.is_equal).then_inc(S.m1, 1)
    v.tensor_scalar(T.e1[:], T.los[:], -1.0, two, op.add, op.is_equal).then_inc(S.m1, 1)
    v.wait_ge(S.g3, 1)
    v.tensor_scalar(T.tb[:], T.th[:], row, None, op.is_ge).then_inc(S.m1, 1)
    v.wait_ge(S.ldw, 16)
    v.tensor_copy(T.wl[:], T.wi[:]).then_inc(S.conv, 1)
    v.wait_ge(S.m1, 3)
    v.tensor_tensor(T.mb0[:], T.tb[:], T.e0[:], op.mult).then_inc(S.m2, 1)
    v.tensor_tensor(T.mb1[:], T.tb[:], T.e1[:], op.mult).then_inc(S.m2, 1)
    v.tensor_tensor(T.blk[:], T.e0[:], T.e1[:], op.add).then_inc(S.m4, 1)
    v.wait_ge(S.m2, 2)
    v.tensor_tensor(T.my0[:], T.e0[:], T.mb0[:], op.subtract).then_inc(S.m3, 1)
    v.tensor_tensor(T.my1[:], T.e1[:], T.mb1[:], op.subtract).then_inc(S.m3, 1)
    v.wait_ge(S.lds0, 16)
    v.tensor_copy(sw[0][half[1], 0:SHARE], sw[0][half[0], 0:SHARE]).then_inc(S.dup, 1)
    v.wait_ge(S.g4, 1)
    v.tensor_scalar(T.tn[:], T.im[:], row, None, op.is_ge).then_inc(S.m5, 1)
    v.wait_ge(S.conv, 1)
    v.wait_ge(S.ldp, 32)
    v.tensor_copy(T.mas[:, KC * rank:KC * rank + KC],
                  T.pepw[:].indirect(T.wl[:, 4 * rank:4 * rank + 4])).then_inc(s2("pg", rank), 1)
    for q in sends:
        v.wait_ge(s2("lst", q), nin[q])
        v.tensor_copy(T["rep%d" % q][:],
                      T.pepw[:].indirect(T["lst%d" % q][:, 4 * rank:4 * rank + 4])).then_inc(s2("pg", q), 1)

    def pack(b):
        v.wait_ge(s2("po", b), 1)
        v.tensor_copy(off[0][:, :, PC * b:PC * b + PC], pa[b % 2][:, 0:2 * PC]).then_inc(s2("pa", b), 1)

    pack(0)
    v.wait_ge(S.m4, 1)
    v.wait_ge(S.m5, 1)
    v.tensor_tensor(T.nb[:], T.tn[:], T.blk[:], op.mult).then_inc(S.m5, 1)
    v.wait_ge(S.m5, 2)
    v.tensor_tensor(T.ny[:], T.blk[:], T.nb[:], op.subtract).then_inc(S.m6, 1)
    v.wait_ge(S.vzer, 2)

    def end_steps(x, t):
        k = R * x + t
        nk, co = T.nk[:, k:k + 1], T.co[:, 2 * k:2 * k + 1]

        def best():
            v.wait_ge(s2("pk", x), N * (t + 1))
            first = BANK - 256 + (2 * E if t else 0)
            v.tensor_reduce(nk, key[x][:, first:first + 256], AxisListType.X, op.max, negate=True).then_inc(s2("red", x), 1)

        def place():
            v.wait_ge(s2("red", x), t + 1)
            for h in range(2) if t < R - 1 else [x]:
                v.tensor_scalar(T.co[half[h], 2 * k:2 * k + 1], T.nk[half[0], k:k + 1], T.nk[half[1], k:k + 1], None,
                                op.subtract).then_inc(s2("cs", x), 1)

        def fetch():
            v.wait_ge(s2("cs", x), min(2 * t + 2, 2 * R - 1))
            if t == 0:
                v.wait_ge(s2("tabs", x), 2)
            v.tensor_copy(wb[x][:], tab[x][:].indirect(co)).then_inc(s2("ws", x), 1)

        def erase_b():
            v.wait_ge(s2("ws", x), t + 1)
            v.tensor_copy(sw[x][:].indirect(wb[x][:, 0:1]), T.zer[:]).then_inc(s2("ka", x), 1)

        def erase_y():
            v.wait_ge(s2("ka", x), t + 1)
            v.tensor_copy(sw[x][:, YO:W].indirect(wb[x][:, 8:9]), T.zer[:]).then_inc(s2("kb", x), 1)

        return [best, place, fetch, erase_b, erase_y]

    def results(x):
        v.tensor_copy(T.winf[half[x], 0:R], T.co[half[x], 2 * R * x:2 * R * x + 2 * R:2]).then_inc(S.fin, 1)
        v.tensor_scalar(T.scf[half[x], 0:R], T.nk[half[1], R * x:R * x + R], -1.0 / F, None, op.mult).then_inc(S.fin, 1)

    v.wait_ge(S.dup, 2)
    for n, (x, t) in enumerate(phases):
        steps = end_steps(*phases[n - 1]) if n else []
        if n == 1:
            v.wait_ge(S.pab, 2)
            v.wait_ge(S.lds1, 32)
        if t == 1:
            v.wait_ge(s2("mv", x), 64)
        if t:
            v.wait_ge(s2("kb", x), t)
        for a, z, got, made, count in pieces(n):
            if n == 0 and a % PC == 0:
                v.wait_ge(s2("pa", a // PC), 1)
            v.wait_ge(got, count)
            v.tensor_tensor(pr[x][:, 16 * a:16 * z], sw[x][:].indirect(off[x][:, 0, a:z]), yg[x][:, 16 * a:16 * z],
                            op.mult).then_inc(made, 1)
            if n == 0 and z in FIRST[1:5:2]:
                pack(z // PC + 1)
            if n == 0 and z == FIRST[4]:
                v.wait_ge(S.pob2, 1)
                v.tensor_copy(off[1][:, :, 0:3 * PC], T.pb[:, 0:6 * PC]).then_inc(S.pab, 1)
                pack(3)
            if n == 0 and z == FIRST[5]:
                v.wait_ge(S.pob3, 1)
                v.tensor_copy(off[1][:, :, 3 * PC:4 * PC], T.key1[:, 0:2 * PC]).then_inc(S.pab, 1)
            if z >= ENDS and steps:
                steps.pop(0)()
    results(0)
    for step in end_steps(1, R - 1):
        step()
    results(1)

    for x in range(2):
        sp.wait_ge(s2("kb", x), R)
        sp.dma_start(T.left[half[x], :], sw[x][half[x], :]).then_inc(S.stl, 16)
    act.wait_ge(S.fin, 4)
    act.dma_start(T.win[:], T.winf[0:128:16, 0:R]).then_inc(S.sts, 16)
    act.dma_start(T.score[:], T.scf[0:128:16, 0:R]).then_inc(S.sts, 16)
    sp.wait_ge(S.stl, 32)
    act.wait_ge(S.sts, 32)
    g.wait_ge(S.lsent, nall)
    g.wait_ge(S.rsent, total)
